import numpy as np, ml_dtypes
CORES = [8,80,112,136,208,240,264,336,368,392,464,496]
N = 12
TOK, K, FT = 512, 3, 1
ROUTE = [[[2,6,11],[4,6,10],[2,9,10],[0,1,10],[0,6,11],[5,6,10],[0,2,9],[0,10,11],[4,9,11],[0,1,6],[2,8,11],[3,6,11],[0,1,2],[2,3,6],[5,8,11],[4,6,7],[7,9,11],[0,1,8],[2,6,11],[6,9,10],[0,1,10],[0,2,10],[0,4,11],[4,5,7],[0,3,10],[2,6,11],[1,6,8],[0,3,5],[3,5,6],[1,7,10],[1,4,8],[4,5,8],[0,1,3],[4,10,11],[5,7,8],[6,8,11],[0,1,9],[3,7,10],[3,8,9],[0,5,10],[0,4,10],[3,7,10],[1,6,7],[2,3,7],[7,8,11],[2,6,7],[1,3,11],[1,4,7],[0,3,7],[4,6,8],[2,8,10],[1,2,6],[2,9,10],[2,8,9],[4,6,10],[1,5,10],[1,2,6],[1,6,9],[2,5,10],[6,8,11],[8,9,11],[0,2,4],[6,8,9],[0,3,10],[2,5,9],[1,4,5],[0,6,11],[3,6,10],[4,5,10],[2,3,8],[3,5,6],[0,1,10],[1,6,7],[4,10,11],[1,4,8],[1,2,10],[2,7,10],[0,3,11],[2,8,11],[0,1,6],[0,6,7],[2,5,7],[3,7,10],[0,5,9],[1,8,10],[0,1,4],[3,5,9],[2,4,6],[0,9,11],[5,7,10],[2,8,11],[1,4,7],[7,9,10],[0,1,9],[0,3,5],[4,9,10],[1,2,6],[0,2,4],[0,1,11],[0,4,8],[0,4,8],[0,2,3],[0,7,10],[0,4,8],[6,10,11],[4,7,10],[6,8,10],[7,10,11],[1,4,9],[0,1,10],[3,6,9],[0,3,7],[1,4,6],[2,4,7],[0,5,6],[0,1,6],[4,9,11],[5,7,10],[3,7,10],[0,4,5],[5,7,8],[0,3,6],[4,8,10],[5,9,10],[5,6,8],[5,8,10],[0,7,10],[2,3,9],[0,10,11],[2,4,10],[6,7,11],[0,5,11],[1,6,11],[0,8,9],[1,3,8],[0,1,2],[3,7,9],[7,8,9],[0,8,9],[0,7,8],[1,7,9],[2,4,10],[0,9,11],[5,8,11],[4,5,7],[0,1,9],[6,7,11],[0,5,6],[0,7,10],[2,3,11],[0,9,10],[6,10,11],[8,9,10],[2,4,10],[0,9,10],[0,1,10],[1,4,8],[0,3,4],[0,6,8],[6,8,10],[0,1,8],[3,6,11],[5,6,10],[6,7,9],[2,9,10],[1,2,7],[1,2,8],[2,8,9],[6,7,8],[3,5,6],[1,6,10],[1,9,10],[0,1,9],[0,1,3],[4,7,10],[4,8,10],[2,9,10],[8,10,11],[2,7,9],[1,4,6],[2,3,5],[0,3,6],[5,6,8],[4,9,10],[1,2,6],[0,6,8],[0,1,3],[2,4,8],[5,6,8],[1,4,5],[1,9,11],[4,10,11],[0,1,10],[2,4,6],[0,3,5],[1,4,8],[2,4,6],[5,6,11],[0,10,11],[0,6,10],[2,7,11],[0,4,11],[2,4,6],[4,7,8],[6,7,10],[2,9,10],[0,5,7],[1,4,11],[1,3,10],[3,6,10],[7,9,11],[1,3,6],[1,3,7],[1,6,11],[4,8,10],[7,8,10],[2,5,8],[3,4,9],[1,2,8],[6,7,8],[3,8,9],[2,4,5],[3,6,10],[1,3,7],[6,8,11],[4,6,9],[6,7,8],[3,5,8],[0,6,10],[4,6,7],[2,3,4],[0,9,11],[1,2,6],[5,8,11],[5,8,11],[4,6,11],[1,4,11],[5,7,11],[5,8,10],[1,2,11],[3,4,11],[4,7,8],[0,2,9],[2,7,11],[3,7,9],[3,8,9],[2,9,10],[3,4,9],[3,7,10],[3,6,9],[4,6,8],[0,1,4],[0,3,5],[4,8,10],[9,10,11],[5,8,10],[4,5,10],[0,2,11],[1,3,4],[4,6,10],[2,4,10],[0,4,11],[1,5,11],[0,3,5],[3,5,10],[2,3,7],[0,10,11],[2,7,8],[3,4,9],[2,4,6],[4,7,11],[3,6,11],[3,7,9],[1,3,8],[3,5,8],[6,7,11],[0,5,7],[7,8,11],[2,3,6],[2,3,10],[2,3,10],[2,5,11],[3,5,11],[0,1,4],[1,3,10],[1,2,11],[0,5,8],[1,6,11],[1,4,10],[0,1,4],[3,4,7],[2,4,10],[1,3,4],[3,4,11],[2,6,10],[2,6,8],[8,10,11],[1,10,11],[2,4,11],[1,3,11],[0,5,6],[1,2,11],[5,6,8],[1,6,7],[1,10,11],[5,7,8],[0,1,7],[0,4,8],[4,8,10],[0,1,11],[0,2,3],[6,7,8],[4,5,10],[0,2,11],[0,7,8],[1,8,10],[2,3,6],[1,5,6],[5,7,11],[4,6,7],[0,9,10],[2,7,9],[0,2,10],[0,2,9],[1,10,11],[4,6,11],[2,7,10],[6,8,10],[5,6,10],[1,2,7],[1,3,11],[6,9,11],[0,6,7],[1,4,7],[4,6,10],[0,1,6],[2,8,9],[1,6,11],[5,6,11],[2,3,10],[2,8,11],[6,8,11],[0,3,7],[2,8,10],[8,9,10],[0,1,8],[1,7,9],[0,2,4],[7,8,11],[2,3,6],[3,5,7],[0,2,7],[5,6,10],[1,6,7],[0,2,5],[2,7,10],[1,3,8],[2,3,10],[3,5,6],[1,6,8],[5,6,10],[1,5,11],[8,9,10],[5,6,11],[2,7,8],[6,9,10],[0,2,10],[0,8,10],[1,3,5],[0,7,10],[0,6,8],[2,5,7],[0,2,10],[3,6,8],[5,9,10],[7,9,10],[0,1,5],[3,6,9],[5,7,8],[2,5,6],[0,4,9],[5,7,9],[0,5,8],[2,6,9],[7,9,11],[5,8,10],[2,4,9],[2,4,10],[1,4,8],[8,9,11],[1,5,6],[4,8,11],[3,6,11],[4,5,7],[3,10,11],[1,5,10],[8,9,11],[1,3,8],[2,4,11],[1,3,6],[3,4,11],[1,4,6],[0,1,10],[1,10,11],[3,4,6],[0,2,6],[3,6,11],[1,5,9],[3,7,9],[1,3,10],[4,5,8],[0,1,2],[5,6,10],[4,5,9],[0,1,4],[1,8,10],[0,7,11],[3,7,9],[0,6,7],[0,3,4],[7,8,11],[6,7,10],[2,6,10],[1,3,10],[2,4,9],[3,8,11],[1,4,10],[1,2,5],[0,1,9],[1,6,8],[1,8,10],[2,5,9],[0,1,11],[5,9,10],[2,4,7],[0,5,6],[2,6,9],[4,7,8],[2,5,8],[1,2,10],[0,6,7],[1,5,6],[5,6,7],[0,6,7],[2,6,10],[2,3,10],[0,1,6],[0,3,7],[0,1,8],[2,5,10],[1,3,11],[4,7,9],[0,1,5],[5,6,11],[3,5,11],[1,5,7],[5,7,9],[4,6,8],[1,3,7],[2,8,9],[2,7,11],[1,4,10],[0,4,8],[4,5,6],[1,9,10],[1,7,11],[2,6,10],[4,8,11],[5,6,9],[5,7,8],[2,4,8],[0,4,9],[4,5,11],[3,4,10],[1,7,9],[3,5,11],[0,1,10],[1,5,6],[5,9,10],[0,6,11],[4,8,9],[1,9,10],[1,4,10],[4,9,11],[2,6,10],[1,6,8],[3,5,10],[1,7,8],[6,9,10],[0,5,7],[5,9,11],[7,8,10],[3,6,11],[0,2,4],[2,5,6],[1,3,4],[2,4,7],[4,5,8],[4,7,11],[2,5,11],[5,6,10],[1,8,10],[1,2,8],[2,5,10],[2,3,10],[1,3,4],[7,9,10],[6,10,11],[5,7,11],[2,7,11],[0,5,10],[6,7,11]],[[1,7,11],[4,7,9],[0,2,10],[5,7,11],[1,3,4],[0,1,3],[0,1,7],[1,8,9],[0,9,10],[4,5,10],[5,7,11],[1,6,10],[4,6,10],[2,4,8],[1,5,7],[0,2,8],[3,6,9],[0,9,11],[1,2,6],[3,5,9],[3,4,10],[2,10,11],[3,10,11],[0,4,11],[0,1,10],[4,7,11],[0,4,6],[0,2,9],[6,8,9],[0,1,4],[3,8,11],[7,8,10],[0,4,8],[0,2,7],[1,3,6],[1,4,10],[4,6,11],[0,1,6],[1,4,9],[1,9,11],[2,9,10],[0,2,8],[1,3,11],[6,7,8],[1,3,10],[2,9,10],[0,1,2],[0,8,11],[0,6,7],[5,8,9],[0,3,11],[3,4,11],[0,2,5],[4,9,10],[4,6,10],[9,10,11],[4,6,10],[2,4,11],[1,4,11],[5,6,7],[3,5,6],[0,1,2],[0,4,10],[6,7,8],[1,9,10],[1,6,7],[3,4,8],[1,2,10],[5,6,11],[0,1,8],[2,6,8],[2,3,4],[0,2,5],[1,6,10],[2,5,7],[0,3,7],[5,7,10],[3,8,11],[4,7,9],[0,1,11],[2,6,11],[2,7,10],[3,8,11],[1,5,8],[4,8,10],[4,8,9],[0,6,7],[4,8,10],[1,4,9],[3,6,8],[0,2,7],[1,4,7],[4,7,10],[1,8,11],[4,7,9],[0,5,9],[3,7,8],[1,5,8],[2,7,9],[5,7,11],[2,6,8],[4,6,7],[2,7,11],[3,6,9],[0,3,9],[3,4,6],[1,5,9],[0,1,3],[5,6,7],[3,5,9],[2,3,9],[0,1,2],[7,8,9],[0,2,7],[3,4,8],[4,5,10],[2,5,10],[0,3,9],[0,10,11],[5,8,10],[0,1,9],[5,6,7],[1,7,11],[2,4,6],[1,3,9],[0,4,9],[2,5,7],[0,2,4],[2,5,9],[6,7,8],[3,4,6],[0,4,7],[4,6,10],[5,7,8],[1,5,10],[1,2,4],[2,8,11],[0,1,9],[5,10,11],[1,3,7],[6,9,10],[1,2,4],[0,5,11],[3,8,11],[1,6,10],[3,6,8],[8,9,10],[2,6,8],[0,4,6],[1,3,5],[1,7,9],[4,6,10],[6,7,11],[0,7,11],[1,3,11],[0,6,8],[0,1,2],[7,9,11],[1,10,11],[3,6,7],[4,10,11],[0,2,11],[3,5,10],[2,3,10],[1,9,11],[0,6,10],[5,6,9],[4,5,6],[1,4,6],[0,4,5],[4,9,10],[4,5,8],[7,8,9],[3,8,10],[0,2,3],[0,5,8],[0,2,9],[0,4,6],[6,9,11],[3,6,8],[7,8,10],[2,6,9],[3,4,10],[2,7,11],[4,5,6],[1,6,11],[3,6,10],[0,3,10],[0,7,11],[2,5,8],[0,1,2],[0,4,8],[0,1,8],[3,4,5],[2,4,11],[1,9,10],[1,2,4],[3,7,10],[2,6,9],[0,5,6],[4,5,9],[3,6,10],[1,3,7],[3,8,9],[3,6,11],[5,6,10],[3,4,5],[0,3,11],[7,8,10],[3,7,11],[2,7,9],[0,7,10],[2,8,9],[0,4,5],[0,1,2],[5,6,11],[0,8,11],[1,4,11],[0,7,10],[7,9,11],[2,3,8],[4,6,10],[3,4,6],[2,3,9],[0,7,9],[0,8,10],[1,2,6],[0,4,7],[0,1,11],[6,7,9],[1,4,11],[1,5,9],[4,7,9],[1,9,10],[3,4,10],[1,3,9],[0,5,8],[0,4,5],[2,4,5],[1,8,9],[3,8,9],[3,9,10],[0,2,3],[0,1,8],[0,3,6],[4,6,10],[1,2,8],[2,9,11],[1,9,10],[3,10,11],[4,7,11],[4,6,10],[0,3,6],[0,5,6],[2,5,7],[2,6,11],[6,8,9],[3,9,10],[1,4,9],[3,4,8],[2,3,8],[1,3,7],[4,10,11],[1,7,11],[2,3,6],[2,6,11],[0,3,6],[1,3,4],[0,4,8],[7,8,10],[5,6,9],[1,5,6],[0,1,6],[2,3,11],[3,6,11],[0,5,11],[1,2,5],[0,3,9],[2,5,8],[0,6,8],[1,2,8],[1,3,8],[2,3,6],[1,8,10],[6,8,10],[0,3,10],[0,5,9],[7,10,11],[0,5,10],[0,6,11],[0,7,8],[0,1,6],[5,8,11],[3,9,11],[7,8,11],[0,2,5],[3,4,11],[2,8,10],[4,8,9],[1,2,9],[0,6,11],[0,3,4],[3,6,10],[2,3,6],[1,2,5],[1,5,6],[4,6,7],[0,2,9],[1,4,5],[7,9,11],[4,8,11],[3,4,11],[0,3,9],[0,1,2],[2,6,8],[4,5,10],[1,5,9],[8,9,11],[2,9,10],[2,4,10],[6,8,10],[0,2,6],[2,4,7],[0,3,11],[0,5,11],[4,6,7],[0,4,10],[6,7,10],[2,4,6],[1,10,11],[4,5,7],[2,5,10],[2,6,11],[0,4,8],[0,1,7],[6,8,10],[0,1,7],[1,3,7],[9,10,11],[7,9,11],[0,3,8],[0,1,9],[3,5,11],[3,7,11],[4,7,10],[3,6,11],[1,5,8],[4,8,10],[1,2,9],[0,5,7],[1,2,10],[1,7,9],[0,3,4],[2,3,9],[4,9,10],[3,4,5],[4,6,9],[8,10,11],[1,3,7],[1,3,4],[4,5,7],[2,7,11],[0,1,2],[0,6,8],[3,5,11],[0,1,8],[5,7,8],[0,3,8],[1,6,10],[1,4,7],[0,8,10],[3,5,8],[3,8,9],[2,3,4],[0,7,10],[0,2,6],[6,10,11],[1,2,10],[0,7,11],[3,8,10],[1,4,5],[0,1,4],[4,5,9],[6,7,9],[5,8,9],[0,1,10],[0,2,3],[3,4,9],[2,3,7],[1,10,11],[3,5,10],[0,4,7],[3,5,6],[6,7,9],[9,10,11],[6,10,11],[1,7,10],[3,5,6],[1,6,8],[0,1,6],[0,10,11],[4,6,10],[5,6,7],[0,3,6],[8,9,11],[0,5,10],[3,4,5],[0,6,8],[0,8,10],[1,3,11],[1,6,7],[3,5,11],[4,5,11],[0,4,10],[2,7,9],[1,8,11],[0,4,6],[4,9,10],[3,5,7],[0,4,11],[2,3,9],[3,7,8],[4,7,10],[2,5,7],[0,5,10],[0,1,2],[4,5,11],[1,2,10],[1,5,7],[4,5,8],[1,2,3],[7,8,10],[0,1,7],[0,7,11],[6,8,10],[1,6,9],[2,7,10],[0,3,8],[1,3,5],[1,3,11],[1,2,3],[0,3,6],[1,2,3],[1,2,8],[2,5,11],[3,6,10],[2,3,7],[0,5,6],[3,6,7],[4,5,10],[2,6,7],[0,1,9],[2,5,6],[1,6,10],[0,2,9],[0,3,11],[7,8,11],[6,9,10],[1,5,11],[0,2,10],[1,2,5],[1,6,9],[7,9,10],[3,7,9],[4,6,10],[0,7,11],[1,4,11],[4,6,10],[3,6,10],[4,5,8],[3,4,10],[4,5,11],[2,8,9],[0,1,3],[0,5,10],[0,2,5],[3,5,10],[4,7,9],[0,3,7],[1,5,9],[0,2,5],[2,3,10],[2,3,9],[4,7,10],[2,3,4],[2,5,6],[5,6,7],[0,9,11],[1,3,7],[5,8,10],[2,9,11],[3,5,11],[1,8,9],[0,7,8],[6,9,10],[2,10,11],[3,9,10],[1,9,11],[0,1,5],[3,5,11],[4,5,7],[3,4,9],[0,3,8],[2,6,10],[1,4,7],[0,5,10],[6,8,10],[0,1,11],[3,4,5],[1,2,3],[4,7,11],[1,5,10]],[[0,4,7],[2,9,11],[4,7,8],[6,7,8],[2,4,5],[0,5,6],[4,7,11],[1,2,8],[0,2,9],[0,5,9],[0,6,11],[0,3,5],[4,8,9],[0,5,7],[3,5,11],[4,8,9],[0,7,9],[0,2,4],[5,6,11],[0,2,9],[0,3,10],[1,4,7],[3,7,11],[1,3,10],[0,2,7],[0,7,9],[1,2,9],[2,7,8],[0,1,4],[7,9,10],[1,5,10],[2,6,10],[2,4,10],[1,6,10],[1,7,11],[0,4,11],[4,8,10],[3,4,8],[3,10,11],[1,6,10],[3,10,11],[1,5,11],[1,7,10],[5,8,9],[0,5,6],[0,6,8],[1,7,8],[1,5,9],[3,5,9],[3,10,11],[0,9,10],[1,3,7],[2,5,10],[0,1,3],[1,3,7],[3,6,11],[1,4,9],[1,5,9],[2,5,8],[1,5,9],[1,8,9],[4,7,11],[6,9,10],[3,6,8],[5,7,9],[1,9,11],[1,6,9],[0,7,11],[6,9,11],[5,7,8],[2,7,11],[2,7,11],[4,6,11],[3,4,9],[4,7,11],[3,8,9],[1,5,10],[0,2,5],[4,7,11],[0,2,11],[0,1,10],[1,3,5],[1,9,11],[2,4,7],[2,5,11],[1,3,8],[3,4,7],[8,9,10],[2,3,6],[0,1,4],[0,4,9],[0,3,6],[0,4,10],[4,8,11],[0,2,5],[0,2,7],[7,9,11],[0,1,3],[5,9,10],[1,5,11],[6,9,10],[0,2,10],[6,8,9],[1,2,4],[5,6,7],[5,9,11],[1,8,11],[6,8,9],[0,6,8],[0,8,11],[4,7,10],[0,4,11],[1,8,10],[3,8,9],[2,6,10],[0,7,8],[2,5,8],[4,7,11],[0,1,6],[7,8,11],[4,6,7],[2,8,9],[7,10,11],[1,2,6],[0,1,5],[3,8,10],[4,5,9],[2,6,9],[0,7,9],[2,4,10],[1,3,9],[0,2,5],[2,6,11],[4,6,9],[0,4,5],[3,5,10],[6,9,11],[2,5,11],[3,5,10],[0,4,8],[1,6,7],[4,5,7],[1,6,9],[2,3,6],[2,6,7],[8,10,11],[6,8,9],[6,7,11],[1,3,7],[1,8,9],[2,6,7],[0,3,9],[2,6,9],[0,2,6],[4,5,9],[2,3,10],[2,3,8],[0,8,9],[5,6,9],[3,8,11],[0,4,9],[0,6,11],[0,5,7],[4,9,10],[0,1,10],[5,8,10],[4,10,11],[2,6,10],[6,7,9],[7,8,11],[0,10,11],[1,3,9],[2,3,5],[1,2,7],[1,9,11],[3,5,6],[2,6,7],[6,7,10],[0,7,9],[4,5,7],[2,8,11],[1,9,11],[3,4,11],[0,3,5],[0,5,11],[2,5,7],[0,1,10],[4,5,9],[2,6,7],[1,5,7],[4,9,11],[1,3,6],[1,4,6],[4,6,9],[3,4,10],[2,8,10],[2,6,8],[2,6,11],[1,6,9],[0,2,10],[6,8,11],[5,7,9],[5,8,9],[0,4,9],[1,6,7],[5,7,8],[6,8,10],[0,1,7],[0,7,10],[0,2,7],[9,10,11],[0,3,6],[7,8,10],[5,7,8],[6,7,10],[0,5,7],[1,2,5],[7,8,9],[1,2,8],[0,1,5],[1,5,10],[2,4,9],[0,3,6],[7,8,11],[2,5,6],[0,6,10],[7,8,10],[2,3,10],[4,8,11],[0,1,11],[0,6,10],[1,5,6],[2,3,11],[3,5,9],[3,6,11],[6,8,11],[4,5,10],[4,5,10],[4,9,10],[1,7,8],[0,8,9],[1,3,11],[0,2,11],[1,9,10],[0,2,10],[2,7,10],[2,4,9],[1,8,9],[3,9,10],[2,10,11],[0,3,7],[3,5,9],[4,7,9],[1,10,11],[1,4,7],[4,5,11],[0,3,10],[0,5,10],[1,3,10],[2,4,5],[1,7,11],[6,10,11],[3,8,10],[1,5,8],[6,8,10],[7,8,10],[0,2,11],[6,8,9],[0,1,10],[0,2,10],[7,9,10],[5,6,11],[2,3,9],[1,7,8],[3,7,8],[1,5,6],[0,2,6],[2,7,11],[2,7,9],[1,3,9],[6,7,11],[7,8,11],[1,5,10],[6,7,9],[1,7,10],[0,3,6],[3,5,8],[0,3,11],[4,6,11],[1,2,7],[1,7,11],[1,3,4],[0,4,11],[4,7,9],[0,8,11],[1,3,4],[5,6,9],[1,6,9],[4,5,9],[1,5,6],[0,4,10],[4,7,8],[5,7,10],[3,8,9],[2,8,10],[1,7,9],[1,8,10],[4,8,10],[6,8,11],[6,9,11],[4,7,8],[7,9,11],[1,4,10],[0,8,11],[2,7,10],[0,3,9],[0,2,5],[2,8,10],[1,4,10],[6,8,9],[2,9,11],[2,8,9],[6,9,11],[2,6,10],[3,4,9],[0,2,7],[8,9,11],[1,3,4],[1,8,9],[3,4,5],[0,1,9],[1,7,9],[1,3,11],[1,5,7],[0,7,8],[0,7,9],[3,5,11],[4,5,9],[2,5,6],[1,6,7],[0,2,7],[1,7,11],[0,6,11],[3,10,11],[1,10,11],[6,7,10],[7,8,11],[0,1,4],[0,6,8],[1,6,10],[3,4,6],[1,10,11],[3,6,8],[2,5,6],[0,3,9],[0,2,11],[1,9,11],[3,5,10],[2,10,11],[4,9,11],[0,8,9],[3,10,11],[0,2,6],[1,10,11],[0,4,10],[1,3,6],[0,4,9],[7,8,9],[0,6,7],[2,4,6],[0,1,8],[2,5,9],[0,5,9],[3,8,10],[2,6,11],[0,8,11],[3,5,9],[0,8,10],[1,6,11],[9,10,11],[0,1,6],[5,6,7],[0,7,11],[4,5,10],[0,10,11],[3,4,8],[2,4,6],[8,9,10],[2,4,11],[2,5,6],[2,6,8],[1,2,7],[2,5,9],[1,8,11],[2,6,9],[3,9,10],[0,5,11],[1,2,10],[0,5,10],[0,2,9],[0,1,2],[1,4,9],[0,1,4],[5,6,11],[3,4,10],[5,6,8],[0,2,6],[4,5,11],[0,6,8],[0,9,10],[0,3,5],[4,6,7],[6,7,10],[2,9,11],[7,9,11],[0,7,8],[2,3,5],[1,7,11],[7,8,11],[7,8,9],[1,5,9],[2,4,9],[1,5,6],[8,9,11],[1,3,6],[2,9,10],[2,3,8],[0,1,9],[3,4,6],[1,4,8],[4,6,10],[4,5,6],[2,7,8],[0,8,9],[0,10,11],[2,5,6],[3,10,11],[3,6,7],[0,1,5],[3,8,11],[3,4,10],[1,6,10],[0,1,11],[0,2,9],[2,4,11],[1,6,7],[0,4,10],[1,3,8],[4,7,11],[7,9,11],[0,9,11],[0,7,11],[4,6,9],[1,5,8],[4,10,11],[5,7,9],[2,7,11],[3,6,8],[1,5,7],[0,5,9],[8,10,11],[1,8,10],[3,4,5],[3,5,9],[0,1,10],[5,10,11],[2,3,11],[1,4,10],[2,8,10],[0,2,10],[1,6,9],[1,4,8],[0,7,10],[2,9,11],[0,6,9],[2,3,8],[3,8,9],[3,10,11],[1,3,11],[0,4,10],[5,6,7],[0,5,11],[2,4,6],[1,7,9],[1,7,11],[7,9,11],[1,5,6],[0,6,11],[4,5,6],[0,2,5],[7,9,11],[1,5,6],[3,7,10],[0,1,8],[5,8,9],[0,10,11],[5,9,10],[3,7,8],[4,8,11],[4,8,11],[3,8,11],[1,6,10],[1,3,7],[2,6,8],[5,8,9],[3,7,11],[1,7,8],[0,3,5],[1,3,10],[9,10,11],[4,9,11],[0,2,8]],[[3,5,8],[3,6,8],[4,6,10],[0,5,8],[5,7,9],[1,4,6],[4,8,9],[2,4,9],[7,8,10],[0,1,10],[2,4,7],[2,3,4],[4,6,10],[3,4,7],[3,5,8],[2,3,6],[0,1,10],[3,6,10],[1,2,3],[1,4,7],[3,7,10],[1,3,4],[0,3,11],[2,5,6],[2,5,9],[2,3,5],[0,3,8],[0,5,7],[2,7,10],[2,5,11],[6,7,11],[0,7,8],[0,6,8],[1,7,11],[1,2,10],[5,8,9],[3,4,11],[0,5,6],[1,5,11],[4,7,8],[0,1,6],[4,6,7],[2,9,10],[2,8,11],[0,4,7],[4,10,11],[4,7,8],[0,4,6],[1,2,6],[2,4,7],[0,5,10],[5,7,8],[4,5,6],[2,6,8],[0,2,4],[0,2,5],[2,9,10],[0,1,7],[4,6,11],[6,8,10],[1,3,5],[0,1,8],[0,1,8],[4,7,9],[0,6,9],[3,7,11],[2,4,11],[4,6,8],[4,8,9],[4,7,9],[0,6,9],[7,9,11],[2,3,11],[0,2,8],[1,5,7],[1,6,9],[3,8,9],[1,2,3],[7,8,10],[1,4,5],[1,8,10],[1,5,6],[0,5,11],[4,9,10],[0,3,9],[5,8,11],[0,6,8],[1,5,11],[0,4,10],[0,3,6],[4,8,11],[0,1,9],[0,8,9],[8,9,11],[2,6,9],[2,3,6],[2,4,7],[5,7,9],[4,5,7],[4,5,11],[3,4,6],[0,1,4],[2,4,6],[0,1,10],[0,6,8],[1,6,11],[3,9,11],[6,8,10],[8,10,11],[6,7,11],[3,6,11],[0,7,10],[0,2,7],[2,7,8],[1,2,4],[5,6,8],[0,5,6],[0,3,5],[2,8,10],[2,9,10],[1,2,7],[2,5,8],[6,9,11],[3,9,11],[1,2,7],[3,5,11],[1,3,11],[0,10,11],[2,3,5],[3,5,9],[0,2,6],[1,8,9],[2,5,9],[1,6,10],[0,1,7],[4,5,10],[4,6,11],[2,4,5],[1,2,6],[0,5,7],[6,10,11],[0,4,6],[0,2,9],[2,3,5],[5,7,9],[6,9,11],[4,9,11],[3,6,7],[2,6,7],[1,2,3],[0,2,3],[6,8,10],[2,4,7],[0,4,8],[2,3,9],[0,8,11],[1,8,10],[4,7,9],[0,2,7],[2,5,6],[3,7,9],[4,6,10],[1,3,8],[0,4,8],[2,6,9],[4,7,9],[0,4,5],[1,5,6],[5,8,9],[1,2,11],[1,4,8],[2,7,10],[7,8,11],[2,3,4],[0,3,10],[5,6,7],[0,5,11],[5,6,8],[1,6,8],[3,4,8],[3,4,6],[5,8,11],[6,10,11],[2,3,6],[0,2,10],[3,8,10],[3,4,8],[2,5,9],[1,4,8],[4,5,6],[6,9,11],[5,7,11],[0,10,11],[2,4,11],[2,7,9],[6,8,10],[1,5,11],[4,8,10],[0,1,3],[2,7,10],[4,8,9],[1,4,9],[1,8,10],[6,8,9],[0,3,4],[0,1,3],[1,2,5],[1,8,11],[0,7,11],[2,7,10],[6,7,9],[5,6,7],[7,9,11],[1,2,10],[6,7,10],[1,4,11],[1,3,11],[2,8,9],[5,6,10],[1,4,6],[0,7,11],[0,1,9],[1,3,8],[0,2,5],[7,8,11],[6,8,10],[6,8,11],[6,10,11],[3,6,7],[1,2,9],[2,4,9],[2,10,11],[1,2,9],[0,4,10],[3,6,10],[2,8,11],[2,3,6],[0,5,6],[5,7,8],[6,7,8],[4,5,8],[1,3,11],[3,4,6],[3,4,5],[5,7,11],[0,2,6],[2,4,5],[1,2,3],[5,7,11],[1,8,9],[2,7,8],[4,8,11],[1,3,8],[0,2,6],[8,10,11],[0,2,3],[2,9,11],[0,3,7],[0,2,3],[0,2,6],[1,10,11],[5,10,11],[1,3,10],[0,1,8],[5,6,9],[0,6,8],[0,1,5],[0,10,11],[2,6,10],[3,4,7],[0,3,4],[1,4,7],[0,1,5],[4,5,9],[8,9,10],[2,3,11],[1,7,10],[0,1,5],[0,2,3],[0,8,9],[4,7,11],[5,8,9],[1,5,6],[4,5,10],[1,4,7],[4,6,9],[0,5,10],[1,5,6],[0,4,7],[2,3,9],[1,5,10],[2,4,11],[3,4,8],[2,5,7],[1,5,9],[0,5,9],[0,7,10],[4,10,11],[2,3,4],[2,4,11],[4,10,11],[1,8,10],[1,5,6],[0,4,11],[4,7,9],[3,7,11],[0,7,9],[5,7,9],[7,8,10],[5,10,11],[0,3,7],[1,6,11],[5,6,11],[4,5,7],[0,6,8],[0,4,9],[8,9,11],[4,6,8],[4,9,11],[4,5,11],[5,7,11],[0,2,7],[0,6,7],[6,7,9],[4,5,7],[4,5,9],[5,7,10],[1,6,10],[1,8,9],[2,3,11],[1,4,9],[4,5,6],[0,1,10],[6,7,11],[3,8,9],[0,3,11],[3,8,11],[0,1,3],[0,5,10],[1,4,11],[0,4,6],[4,6,11],[4,6,9],[3,5,7],[3,7,10],[1,5,6],[3,5,10],[3,4,5],[6,7,9],[0,3,7],[6,8,10],[0,9,10],[0,9,11],[2,6,11],[2,8,10],[5,6,11],[6,7,9],[1,8,9],[2,3,9],[3,5,10],[3,4,6],[1,7,11],[2,9,11],[5,8,10],[2,4,6],[0,4,11],[0,10,11],[2,3,4],[0,1,5],[4,6,10],[2,3,10],[1,4,6],[1,3,5],[5,10,11],[1,4,6],[1,9,10],[0,5,7],[2,6,9],[0,9,11],[0,9,10],[5,8,10],[1,5,11],[0,4,11],[3,5,7],[0,4,8],[2,8,11],[5,7,11],[0,1,4],[2,3,9],[0,2,6],[2,5,8],[0,5,10],[2,7,10],[5,6,10],[2,4,6],[3,7,10],[2,8,9],[2,7,8],[1,7,10],[5,6,11],[8,9,11],[1,7,9],[7,8,9],[2,4,5],[1,8,9],[1,2,8],[9,10,11],[1,4,10],[2,7,10],[6,8,10],[0,1,6],[1,6,7],[0,1,4],[0,3,9],[1,2,5],[0,5,6],[3,9,11],[4,5,11],[4,7,10],[2,6,10],[4,5,7],[0,4,6],[2,6,9],[0,5,8],[0,3,5],[0,1,9],[0,6,11],[1,4,6],[8,9,11],[2,3,9],[6,9,11],[9,10,11],[0,3,8],[4,6,9],[1,4,5],[0,10,11],[1,4,7],[3,8,11],[3,4,6],[3,5,7],[0,1,4],[6,7,10],[0,1,7],[7,9,10],[2,6,9],[0,7,8],[6,7,8],[0,4,10],[2,3,10],[3,6,8],[4,8,9],[1,7,10],[1,6,9],[2,5,7],[1,3,10],[4,5,7],[3,7,8],[1,3,10],[1,6,8],[2,4,9],[0,6,11],[0,6,9],[7,9,11],[3,7,9],[0,5,11],[2,3,7],[0,3,5],[1,5,10],[1,4,7],[0,3,7],[4,6,8],[2,3,10],[2,3,6],[5,8,10],[2,4,6],[0,1,6],[1,2,3],[0,10,11],[2,5,10],[1,7,9],[0,8,9],[8,9,10],[6,8,9],[6,8,11],[0,6,8],[5,6,9],[1,2,3],[0,1,10],[2,6,10],[4,5,11],[3,6,10],[4,9,10],[4,8,11],[0,2,9],[3,9,10],[1,3,4],[6,9,10],[0,9,11],[2,7,11],[6,7,10],[0,1,7],[3,4,6],[2,4,8],[0,1,7],[2,5,6],[0,2,9],[1,3,7],[6,7,11],[8,9,11],[0,1,2],[2,10,11],[1,7,11]],[[4,6,11],[1,7,9],[1,5,7],[1,7,10],[1,3,10],[5,8,11],[1,2,9],[1,4,8],[2,3,11],[3,7,11],[5,6,10],[1,3,10],[0,2,3],[0,6,9],[1,9,10],[0,10,11],[2,9,11],[1,3,9],[6,7,9],[1,7,10],[4,7,10],[1,4,7],[2,3,11],[0,8,10],[0,1,11],[0,4,5],[3,4,10],[1,7,8],[3,6,10],[0,10,11],[4,7,10],[0,4,11],[0,3,6],[2,8,10],[5,8,10],[1,5,8],[1,7,10],[5,7,10],[3,5,8],[2,5,10],[4,9,10],[4,9,11],[0,2,11],[0,3,7],[4,9,10],[5,6,10],[2,6,8],[1,7,11],[4,6,11],[3,8,11],[4,5,11],[0,3,8],[0,8,10],[2,9,11],[2,3,8],[0,5,11],[6,7,11],[6,7,10],[4,7,8],[1,2,4],[3,8,9],[4,10,11],[7,9,10],[0,4,10],[5,8,10],[0,5,7],[3,4,7],[0,4,10],[3,4,11],[1,3,9],[2,4,8],[0,5,7],[0,8,9],[0,2,9],[1,4,7],[2,6,7],[3,7,11],[1,9,11],[1,2,7],[3,5,9],[1,2,4],[0,7,10],[1,3,4],[5,7,11],[1,3,10],[3,8,9],[0,3,6],[2,9,10],[5,8,11],[1,3,11],[0,1,7],[1,8,11],[0,2,4],[0,3,4],[2,7,11],[2,4,6],[1,7,8],[0,1,5],[1,6,10],[1,6,10],[1,3,5],[1,4,11],[3,5,7],[0,4,5],[6,7,11],[2,5,6],[0,4,11],[4,10,11],[2,7,11],[7,8,10],[1,8,9],[1,4,8],[1,7,9],[2,9,11],[3,5,9],[0,4,5],[2,5,8],[3,8,9],[1,5,7],[2,3,11],[0,5,10],[0,1,7],[1,3,5],[2,9,10],[0,8,11],[2,3,10],[0,1,10],[3,6,9],[3,6,11],[2,6,11],[0,3,11],[1,6,8],[1,2,5],[2,3,4],[1,4,6],[3,5,8],[0,5,8],[3,5,9],[4,6,10],[0,1,4],[5,8,11],[1,4,10],[1,4,11],[3,5,10],[3,4,10],[2,3,7],[0,8,10],[2,4,7],[0,7,10],[0,4,10],[0,7,10],[8,10,11],[0,4,11],[5,6,10],[5,9,10],[2,6,11],[6,7,8],[9,10,11],[0,7,11],[1,3,9],[5,8,11],[1,7,8],[7,8,9],[3,4,5],[0,2,3],[5,9,10],[4,7,9],[1,3,4],[2,9,10],[2,7,9],[1,9,10],[0,3,6],[1,8,9],[0,8,9],[3,4,8],[2,8,11],[2,3,10],[0,5,6],[2,4,7],[0,6,11],[2,5,8],[1,6,10],[0,1,5],[3,5,10],[1,3,6],[6,7,8],[2,4,10],[2,3,5],[1,3,6],[2,3,4],[3,6,7],[2,6,10],[2,9,10],[1,5,7],[0,8,11],[4,7,9],[4,10,11],[5,7,9],[4,6,11],[3,7,10],[0,2,9],[1,9,10],[4,9,10],[5,8,11],[0,5,9],[7,8,11],[0,1,6],[1,6,9],[5,6,11],[1,2,6],[0,4,11],[2,10,11],[0,10,11],[8,9,10],[5,8,11],[1,3,9],[1,8,9],[0,3,4],[0,1,6],[1,5,6],[1,2,4],[0,7,8],[2,5,7],[1,3,7],[0,2,9],[3,5,8],[8,9,10],[3,6,10],[1,5,8],[0,5,9],[2,5,11],[6,9,11],[3,10,11],[3,4,6],[1,7,11],[1,4,11],[0,5,9],[0,2,3],[5,6,11],[4,6,7],[2,6,11],[1,2,4],[4,5,10],[1,3,5],[0,1,8],[6,7,11],[1,3,6],[1,6,8],[2,5,11],[6,7,10],[0,2,4],[1,4,7],[1,2,10],[4,6,10],[0,4,8],[0,6,9],[4,5,10],[5,6,9],[3,10,11],[2,10,11],[4,7,11],[6,9,11],[4,8,11],[1,8,10],[3,5,8],[2,3,4],[2,3,8],[1,5,6],[3,5,7],[0,8,11],[4,5,8],[0,10,11],[1,8,10],[2,10,11],[7,9,10],[2,6,7],[3,8,11],[2,5,11],[0,7,11],[4,7,11],[6,8,11],[1,5,9],[0,1,11],[0,1,3],[5,8,11],[3,8,11],[1,2,9],[3,9,10],[2,5,7],[3,7,8],[4,10,11],[4,9,10],[2,9,10],[0,4,5],[2,10,11],[1,5,10],[1,3,9],[2,4,10],[0,2,9],[4,6,11],[1,6,11],[0,1,7],[4,8,11],[2,6,9],[1,2,10],[1,4,8],[9,10,11],[4,5,7],[5,6,11],[4,8,11],[1,4,6],[6,7,11],[0,7,9],[2,7,10],[2,3,6],[0,1,5],[5,6,9],[2,4,7],[4,5,11],[1,4,8],[0,10,11],[3,9,11],[1,5,6],[4,6,8],[1,5,9],[0,6,9],[0,3,8],[1,5,7],[2,4,7],[0,6,7],[0,2,11],[1,2,11],[2,8,11],[6,7,9],[1,4,9],[2,8,9],[1,3,9],[2,4,8],[2,5,11],[1,7,11],[1,9,10],[0,2,10],[1,2,11],[0,4,10],[5,7,11],[2,9,10],[1,6,10],[1,7,10],[0,4,11],[2,7,11],[0,2,11],[0,1,6],[1,3,10],[8,9,11],[1,5,6],[3,4,6],[1,3,9],[2,8,9],[4,8,10],[4,7,8],[2,3,10],[0,7,9],[0,5,10],[2,7,10],[1,3,9],[1,7,8],[5,9,11],[5,6,10],[2,3,5],[0,5,9],[7,9,10],[1,9,10],[2,5,7],[1,6,10],[1,4,7],[0,2,9],[0,5,10],[1,2,4],[1,3,4],[5,7,8],[0,6,9],[2,7,8],[4,8,9],[2,3,7],[3,4,7],[3,4,9],[1,9,11],[0,4,7],[1,3,10],[4,6,8],[3,5,6],[5,8,11],[5,10,11],[5,8,11],[0,9,11],[0,5,6],[3,6,11],[1,3,6],[7,8,11],[4,9,10],[3,5,9],[1,3,11],[1,4,9],[0,6,11],[0,8,11],[2,3,9],[5,8,9],[0,6,7],[3,8,11],[0,5,11],[2,3,5],[3,5,7],[0,1,7],[1,4,7],[1,6,11],[1,8,9],[1,4,5],[0,5,9],[0,2,4],[2,6,7],[4,5,11],[0,5,9],[0,9,10],[1,6,7],[2,7,9],[1,8,9],[5,6,11],[2,3,5],[0,2,7],[5,6,10],[0,10,11],[4,5,9],[5,8,10],[1,6,10],[0,2,3],[3,9,10],[2,6,11],[2,5,8],[0,5,10],[4,7,9],[0,3,5],[3,7,11],[3,7,8],[2,6,8],[0,9,10],[1,3,11],[0,1,6],[0,1,8],[3,9,10],[3,7,8],[0,2,9],[0,2,10],[1,3,9],[2,4,9],[3,5,10],[5,7,11],[1,10,11],[1,5,8],[1,3,8],[4,9,11],[2,5,10],[2,6,8],[0,4,6],[6,9,11],[3,9,10],[6,7,8],[7,8,9],[3,7,11],[2,8,10],[4,8,11],[0,7,10],[0,7,8],[0,6,10],[3,5,6],[1,3,4],[0,3,8],[2,3,8],[3,5,10],[3,5,9],[0,1,3],[7,9,10],[0,1,11],[1,4,6],[2,10,11],[3,4,9],[4,7,11],[3,5,7],[0,7,10],[3,5,7],[2,4,6],[8,10,11],[4,5,9],[3,4,11],[1,4,7],[0,6,11],[8,10,11],[1,4,5],[0,3,9],[1,3,9],[0,2,11],[1,10,11],[2,4,5],[0,5,6],[1,4,6],[4,6,11],[2,7,10],[0,9,10],[1,5,8],[3,9,11],[4,6,11],[3,4,8],[8,10,11]],[[1,6,9],[0,6,11],[2,4,7],[3,5,8],[5,7,9],[5,6,10],[0,1,10],[5,6,11],[7,9,11],[0,3,10],[1,3,8],[0,8,11],[1,7,11],[1,3,8],[8,10,11],[1,2,6],[8,10,11],[3,4,7],[0,2,8],[0,7,11],[0,9,10],[2,3,7],[4,9,10],[2,3,9],[0,4,10],[8,9,11],[6,7,11],[6,9,10],[1,2,10],[2,3,6],[4,9,11],[5,6,11],[6,7,10],[4,8,9],[1,4,10],[0,2,6],[3,4,9],[2,4,8],[2,5,9],[1,7,9],[0,2,4],[0,2,8],[5,7,10],[4,5,11],[2,9,10],[0,8,11],[0,4,5],[2,9,10],[1,2,7],[0,2,11],[5,7,8],[2,3,7],[1,4,5],[0,7,11],[1,4,7],[1,4,5],[1,3,6],[6,7,10],[4,8,11],[5,8,10],[2,8,9],[5,7,11],[1,2,6],[0,1,9],[2,8,9],[1,4,7],[3,8,9],[4,7,10],[1,2,9],[0,1,7],[0,6,9],[4,6,9],[3,6,11],[3,5,7],[7,8,11],[1,2,11],[5,6,7],[0,7,9],[3,4,9],[0,4,10],[6,10,11],[3,6,8],[1,4,6],[4,7,8],[1,2,6],[5,6,7],[6,8,10],[1,5,11],[6,7,8],[5,8,11],[1,6,10],[4,7,9],[1,8,10],[2,7,8],[1,4,10],[1,3,11],[4,7,8],[6,10,11],[0,1,6],[1,3,9],[0,5,8],[3,8,9],[3,7,9],[2,6,11],[4,9,10],[3,5,8],[4,8,10],[6,8,10],[4,10,11],[0,2,10],[2,3,6],[0,1,2],[1,4,5],[1,6,7],[5,6,7],[5,6,11],[5,10,11],[3,4,9],[2,4,5],[2,3,11],[2,6,8],[3,4,5],[2,6,9],[1,7,11],[3,7,11],[1,3,4],[4,6,7],[1,4,8],[3,6,8],[0,3,11],[3,6,8],[3,8,9],[1,4,7],[3,6,8],[2,5,11],[1,3,4],[0,5,7],[4,9,11],[0,8,9],[6,9,10],[0,4,6],[3,4,7],[3,7,8],[2,5,8],[3,4,11],[2,8,10],[0,3,11],[0,5,8],[3,4,7],[3,5,6],[0,5,9],[2,7,8],[4,6,10],[5,7,11],[7,8,10],[2,10,11],[0,5,6],[5,6,7],[5,6,7],[1,2,7],[6,8,10],[3,5,10],[3,8,10],[1,3,9],[4,5,6],[2,4,6],[2,6,8],[3,4,10],[5,7,10],[0,2,9],[5,6,10],[2,4,5],[1,2,5],[1,9,11],[0,3,11],[0,10,11],[0,3,4],[0,3,10],[1,7,11],[2,6,11],[1,8,9],[5,9,10],[5,7,11],[0,2,9],[4,6,8],[5,9,11],[0,2,3],[1,2,4],[0,5,11],[0,1,2],[1,5,11],[0,3,9],[1,3,8],[3,7,10],[0,7,9],[4,8,11],[4,7,10],[5,6,7],[0,3,11],[0,2,6],[1,2,10],[1,9,10],[1,2,9],[0,2,11],[1,3,10],[1,4,8],[3,5,11],[1,2,9],[3,4,8],[3,4,5],[6,7,9],[0,2,4],[6,10,11],[1,5,7],[0,4,9],[3,7,10],[1,5,9],[1,7,9],[1,7,9],[0,4,7],[5,8,10],[4,5,6],[1,2,7],[8,9,11],[5,9,10],[6,7,11],[0,1,11],[0,8,11],[2,10,11],[0,5,10],[4,6,7],[4,8,9],[1,2,7],[0,4,7],[4,5,6],[2,3,10],[0,8,10],[8,9,10],[7,9,11],[1,4,7],[6,9,10],[0,4,5],[0,3,9],[0,2,3],[1,4,9],[0,2,8],[8,10,11],[1,2,11],[2,3,7],[2,3,10],[1,4,11],[3,5,10],[7,8,11],[3,8,11],[6,9,11],[3,7,9],[0,3,4],[7,8,10],[2,4,8],[1,4,8],[0,9,10],[6,7,10],[2,4,9],[1,7,11],[3,4,7],[3,5,8],[1,2,5],[5,7,8],[1,3,5],[0,4,9],[2,7,9],[1,7,11],[3,6,7],[3,4,6],[0,1,2],[4,8,10],[4,6,8],[1,10,11],[3,5,6],[1,4,6],[1,8,10],[1,2,6],[4,7,10],[6,7,8],[0,4,11],[1,8,10],[4,5,10],[5,6,11],[1,4,9],[2,7,10],[1,6,9],[1,7,10],[0,1,11],[1,3,8],[5,7,11],[9,10,11],[1,10,11],[4,5,7],[3,4,6],[5,7,11],[6,8,10],[2,7,8],[4,5,11],[0,7,8],[0,4,10],[1,6,8],[5,7,8],[0,1,9],[0,5,9],[3,7,8],[1,3,8],[6,7,11],[1,6,9],[6,9,10],[5,10,11],[0,2,6],[6,9,11],[3,4,5],[2,7,9],[0,2,4],[2,7,9],[0,5,6],[1,5,9],[0,7,8],[0,2,3],[2,3,6],[2,8,11],[0,8,9],[2,3,6],[1,2,5],[1,2,7],[3,8,9],[2,5,11],[3,4,11],[6,9,11],[5,7,11],[0,3,11],[1,3,9],[0,6,8],[1,6,9],[6,8,10],[7,8,10],[0,1,9],[2,3,5],[0,2,11],[5,6,9],[4,6,9],[4,7,11],[4,7,8],[6,7,9],[2,5,11],[0,3,9],[3,4,9],[3,7,10],[4,5,6],[0,3,11],[0,2,5],[2,6,11],[6,7,11],[5,7,9],[3,4,10],[1,5,8],[1,2,9],[5,10,11],[5,6,10],[1,4,8],[0,2,9],[5,7,11],[1,3,8],[1,3,5],[8,10,11],[2,7,10],[3,10,11],[1,6,8],[5,8,10],[2,5,10],[6,8,10],[4,7,11],[7,9,11],[2,4,7],[8,9,10],[0,5,7],[3,7,11],[0,1,9],[0,5,10],[4,7,11],[5,7,9],[5,8,10],[0,6,11],[2,8,11],[6,7,11],[4,6,9],[2,3,8],[2,7,9],[2,3,4],[2,4,5],[6,7,9],[1,2,3],[0,1,11],[4,7,11],[1,4,7],[0,3,10],[4,7,8],[0,1,5],[1,2,9],[3,4,9],[1,7,9],[3,6,9],[5,6,11],[5,6,10],[1,3,6],[0,4,7],[2,7,9],[3,5,6],[4,7,9],[0,9,11],[3,5,7],[0,6,10],[1,5,6],[0,6,10],[1,6,7],[8,10,11],[2,7,11],[0,6,9],[2,4,9],[0,6,11],[1,7,11],[1,4,9],[1,5,6],[3,8,10],[1,7,11],[2,7,11],[7,9,11],[4,9,10],[4,6,9],[0,1,6],[1,4,5],[2,9,10],[1,4,11],[5,9,10],[0,3,10],[3,5,8],[3,8,10],[2,4,8],[1,6,11],[0,5,7],[0,9,11],[3,5,8],[2,8,9],[4,6,8],[1,5,9],[2,7,10],[0,7,8],[4,5,9],[4,7,8],[6,8,10],[1,3,9],[0,4,10],[4,8,10],[2,3,5],[1,2,6],[1,2,3],[2,4,5],[6,9,11],[3,9,11],[7,10,11],[6,7,11],[0,2,10],[3,5,10],[6,7,9],[2,3,6],[1,7,9],[3,5,10],[2,6,8],[3,4,5],[2,3,10],[6,8,11],[0,5,11],[1,4,6],[0,3,6],[1,6,9],[0,2,5],[6,7,11],[6,9,10],[3,6,10],[2,3,10],[5,6,11],[2,4,9],[1,8,9],[1,4,6],[5,8,9],[1,6,10],[0,2,7],[0,5,6],[0,6,9],[1,8,11],[0,7,9],[0,7,10],[3,4,7],[0,2,6],[4,8,10],[2,7,10],[3,7,10],[6,9,11],[3,4,5],[4,7,11],[0,2,3],[1,5,8],[2,3,4],[4,5,7],[4,6,11],[0,1,4]],[[6,9,10],[4,5,11],[0,7,9],[3,6,10],[0,2,6],[1,3,11],[1,3,6],[0,6,11],[3,5,9],[3,5,9],[0,5,11],[1,2,11],[1,3,10],[2,7,11],[0,1,9],[3,7,11],[7,8,11],[2,5,10],[0,10,11],[2,4,8],[1,7,9],[0,1,6],[5,8,11],[1,6,8],[4,6,8],[7,8,11],[3,4,7],[6,8,10],[4,5,6],[4,5,6],[1,7,10],[3,8,11],[1,2,8],[0,2,6],[6,7,9],[3,4,9],[5,9,11],[4,10,11],[0,4,7],[2,6,8],[1,4,5],[2,7,11],[3,6,10],[3,4,10],[3,5,8],[2,4,5],[3,4,5],[1,2,6],[3,8,10],[5,6,10],[8,10,11],[1,2,8],[0,2,7],[6,7,10],[0,2,4],[0,1,7],[5,9,10],[2,8,11],[1,4,5],[0,1,10],[0,1,9],[2,3,11],[6,7,9],[0,3,5],[6,9,10],[3,5,9],[4,5,10],[5,10,11],[3,6,10],[1,7,10],[0,5,7],[2,3,9],[3,8,10],[0,1,6],[2,6,7],[1,8,11],[3,8,10],[3,4,6],[5,7,10],[2,7,8],[0,3,5],[0,3,11],[2,3,11],[2,6,8],[4,5,7],[6,8,10],[0,2,7],[0,1,6],[0,4,7],[3,5,11],[0,2,4],[3,4,10],[1,8,11],[0,6,11],[0,2,7],[2,6,8],[1,3,8],[0,1,7],[2,3,5],[2,7,9],[3,4,11],[7,8,10],[5,7,8],[0,3,11],[2,9,11],[4,8,11],[1,6,10],[6,8,10],[2,4,10],[0,7,8],[0,2,6],[6,7,10],[2,3,4],[0,1,7],[1,5,9],[1,3,9],[1,8,10],[0,4,5],[0,5,11],[2,5,8],[0,4,8],[1,5,9],[1,3,10],[1,2,5],[1,7,9],[0,4,6],[4,7,9],[5,8,10],[0,3,10],[1,3,4],[0,6,7],[8,9,11],[2,10,11],[1,6,11],[8,9,11],[0,2,11],[1,4,6],[3,9,11],[3,6,9],[5,10,11],[1,2,8],[3,8,10],[1,3,10],[3,6,11],[0,5,10],[0,2,7],[3,8,10],[3,4,7],[1,3,8],[2,3,8],[4,6,7],[1,2,8],[2,4,10],[4,7,10],[1,3,7],[1,4,9],[0,10,11],[4,8,9],[0,6,7],[0,1,10],[3,6,10],[6,10,11],[0,7,10],[0,6,9],[4,7,11],[0,2,4],[4,5,8],[4,5,7],[4,7,9],[0,4,11],[2,8,11],[0,4,10],[5,7,9],[6,8,9],[6,8,9],[0,5,10],[3,5,9],[0,3,8],[1,2,6],[1,4,7],[0,5,9],[2,6,9],[1,2,4],[1,3,5],[2,7,11],[2,8,10],[1,2,10],[2,7,10],[5,9,10],[1,2,8],[0,9,10],[6,7,8],[1,2,8],[0,1,11],[3,8,9],[1,3,5],[7,9,11],[5,6,10],[0,2,6],[2,3,5],[0,3,11],[1,7,8],[4,5,7],[0,2,7],[6,10,11],[0,3,10],[4,5,11],[2,4,9],[0,2,6],[1,6,7],[0,6,10],[2,8,10],[0,4,6],[1,10,11],[1,7,10],[0,5,10],[2,6,7],[1,5,9],[5,6,7],[2,5,7],[1,9,11],[6,9,10],[0,1,6],[3,4,8],[3,7,11],[1,2,3],[0,9,10],[0,3,11],[1,4,11],[2,4,8],[3,4,8],[8,9,10],[0,10,11],[5,7,9],[1,6,7],[4,6,7],[4,6,7],[4,5,7],[7,8,11],[0,4,10],[0,8,11],[5,6,9],[0,7,8],[0,2,9],[1,2,4],[2,5,7],[1,5,10],[7,8,9],[2,3,7],[0,5,10],[0,5,9],[3,5,11],[0,7,9],[0,3,8],[5,6,10],[0,1,3],[0,2,10],[8,10,11],[1,5,8],[2,8,9],[5,8,9],[4,5,10],[0,6,10],[0,3,8],[0,2,7],[4,9,10],[7,8,10],[4,5,10],[0,3,5],[0,1,8],[5,6,7],[0,8,9],[1,3,7],[3,5,11],[3,5,8],[5,9,10],[0,2,8],[1,4,8],[2,5,6],[9,10,11],[4,9,10],[4,7,8],[1,2,3],[0,1,6],[0,7,8],[0,2,3],[2,6,9],[0,4,9],[0,4,8],[0,4,8],[1,5,8],[4,8,10],[2,3,6],[4,5,6],[2,3,7],[4,5,6],[4,9,11],[1,3,11],[7,9,11],[5,10,11],[0,1,4],[4,6,11],[1,7,10],[4,7,9],[2,6,11],[0,2,6],[2,3,8],[2,6,8],[0,4,11],[2,3,9],[0,1,4],[6,8,10],[2,6,8],[2,5,9],[2,3,8],[0,6,7],[3,7,10],[2,5,10],[1,9,11],[5,8,9],[1,4,6],[0,4,10],[0,7,10],[2,6,7],[5,6,8],[1,3,8],[3,7,10],[0,1,7],[0,2,8],[1,3,4],[4,5,6],[1,9,11],[3,7,11],[0,1,3],[1,3,6],[0,2,11],[0,1,3],[1,3,9],[1,3,10],[1,2,6],[0,6,10],[3,6,8],[5,6,11],[5,6,10],[0,7,8],[5,7,8],[0,6,11],[3,9,10],[5,7,8],[8,9,11],[0,4,6],[2,5,10],[5,9,11],[4,6,11],[0,1,5],[5,6,10],[5,8,11],[0,2,3],[0,2,11],[3,5,8],[6,9,10],[0,2,9],[1,5,6],[0,1,9],[3,6,9],[5,6,8],[1,7,8],[4,5,11],[0,5,11],[1,8,11],[1,2,11],[5,7,9],[0,2,3],[1,4,7],[0,4,10],[4,8,9],[0,2,7],[4,5,11],[3,5,11],[1,3,11],[0,3,4],[3,6,7],[0,2,4],[2,9,11],[1,3,8],[3,6,8],[5,8,10],[2,8,9],[4,7,10],[0,4,9],[2,3,8],[1,3,8],[2,9,11],[0,6,11],[5,8,10],[5,9,11],[1,3,9],[2,3,10],[4,8,9],[1,3,4],[0,5,6],[7,9,11],[2,6,7],[3,7,10],[0,6,8],[4,5,11],[6,8,9],[6,8,11],[0,8,10],[1,2,4],[6,8,10],[2,5,11],[2,7,11],[0,2,3],[0,4,7],[1,5,10],[1,3,6],[3,7,11],[3,6,11],[2,6,9],[2,7,8],[2,3,6],[1,6,7],[6,9,11],[0,1,9],[2,9,11],[2,6,8],[1,5,7],[2,4,10],[1,3,6],[0,7,10],[0,4,8],[0,4,8],[0,7,11],[1,3,10],[0,8,10],[4,5,8],[3,4,10],[3,6,7],[4,5,9],[4,5,8],[0,1,7],[5,6,7],[8,9,11],[5,9,10],[5,8,9],[1,6,10],[3,4,6],[6,9,11],[5,8,10],[5,8,10],[0,3,7],[0,8,10],[6,7,10],[5,6,9],[0,2,8],[2,3,7],[1,7,9],[3,8,11],[2,7,11],[6,7,11],[3,7,9],[1,2,4],[8,9,11],[2,3,5],[1,5,9],[3,6,10],[2,3,10],[2,6,8],[4,5,11],[1,3,8],[0,7,11],[0,8,11],[5,8,11],[2,4,7],[0,7,8],[1,9,11],[0,2,6],[0,2,4],[4,5,9],[1,9,11],[5,8,9],[2,7,10],[7,9,10],[0,8,10],[3,8,10],[2,5,6],[5,7,8],[0,1,4],[6,7,8],[4,5,7],[1,3,7],[0,2,7],[0,1,3],[1,4,10],[2,3,6],[1,7,11],[9,10,11],[1,6,8],[3,5,8],[0,4,10],[0,2,8],[1,3,9],[3,4,7],[9,10,11],[1,2,8],[1,8,11],[4,5,11],[0,7,10],[1,6,10],[2,6,8],[1,3,5]],[[3,6,11],[1,2,9],[2,6,7],[1,9,11],[3,5,6],[2,8,9],[0,2,8],[4,8,11],[1,5,6],[0,6,10],[1,2,3],[1,5,11],[1,4,7],[0,6,10],[4,6,10],[3,8,9],[0,2,11],[0,1,11],[1,5,7],[6,9,11],[5,8,11],[5,7,8],[0,3,10],[0,7,8],[2,3,9],[5,8,11],[3,6,7],[2,3,6],[2,7,8],[2,4,11],[0,8,9],[6,8,11],[6,10,11],[7,10,11],[0,1,3],[0,2,3],[2,6,11],[3,8,10],[0,3,5],[1,2,9],[7,8,9],[2,8,11],[0,2,8],[1,5,6],[0,6,11],[4,7,11],[6,8,10],[2,6,10],[0,7,11],[2,4,6],[3,5,8],[2,3,11],[7,9,11],[1,5,6],[1,2,3],[2,3,6],[3,5,9],[3,6,7],[0,1,3],[0,4,5],[1,6,9],[4,5,9],[0,6,11],[0,9,10],[0,2,10],[0,3,11],[1,10,11],[5,6,11],[2,6,7],[0,4,6],[0,4,7],[0,4,6],[0,3,8],[0,4,6],[1,6,9],[3,7,8],[0,1,8],[2,5,9],[5,9,11],[1,9,10],[3,4,5],[4,7,11],[3,6,8],[3,9,11],[0,3,8],[3,5,7],[2,4,5],[4,7,10],[1,3,6],[1,5,9],[2,3,10],[0,2,5],[2,3,11],[2,3,4],[2,10,11],[3,4,8],[1,4,7],[1,4,6],[5,7,11],[4,6,8],[1,4,7],[0,7,10],[2,7,8],[0,1,9],[2,7,10],[6,7,9],[1,4,5],[5,7,10],[4,5,8],[1,4,11],[2,5,6],[2,4,10],[4,7,9],[2,6,9],[4,7,8],[4,5,11],[0,2,10],[2,3,9],[6,10,11],[0,7,8],[4,7,9],[5,7,11],[0,6,7],[2,5,9],[1,5,11],[2,9,10],[2,3,5],[6,8,10],[7,9,11],[0,5,6],[0,5,6],[2,4,11],[4,9,11],[0,10,11],[4,7,9],[4,6,7],[0,5,8],[0,3,11],[6,8,10],[1,5,6],[0,6,11],[0,4,10],[4,9,11],[3,7,11],[7,8,9],[1,8,9],[0,5,9],[3,4,8],[1,5,9],[3,8,10],[3,4,5],[4,5,6],[2,4,5],[4,5,8],[0,2,3],[0,6,8],[0,2,9],[0,6,11],[0,8,10],[4,5,8],[2,7,9],[6,8,9],[1,4,5],[0,1,4],[6,9,10],[1,4,7],[0,1,5],[0,4,8],[3,5,6],[1,4,6],[3,9,10],[0,1,9],[5,7,9],[0,6,7],[1,3,11],[1,6,11],[3,4,11],[0,2,6],[2,4,5],[4,6,9],[5,7,8],[1,2,11],[1,4,11],[6,7,9],[2,7,11],[1,2,11],[3,5,10],[1,3,11],[2,4,8],[2,4,10],[2,6,11],[1,5,10],[4,9,11],[0,5,6],[0,1,8],[2,6,11],[1,2,11],[0,7,10],[2,3,8],[0,6,9],[4,7,10],[1,5,10],[0,5,7],[4,7,9],[2,7,8],[7,9,10],[1,6,11],[1,6,11],[4,9,10],[4,6,7],[4,5,8],[1,7,10],[3,6,10],[7,8,9],[4,7,11],[7,8,11],[8,9,11],[3,9,11],[4,6,8],[2,6,11],[2,4,8],[0,4,9],[7,10,11],[5,8,9],[2,4,10],[3,8,9],[0,1,6],[2,9,11],[1,2,4],[0,1,3],[0,1,11],[4,5,10],[5,8,9],[4,10,11],[1,3,5],[0,4,8],[3,6,7],[1,4,9],[0,2,7],[3,9,11],[3,7,11],[0,3,7],[2,8,10],[0,7,9],[3,7,11],[3,8,11],[4,6,9],[1,6,9],[3,5,9],[0,5,6],[2,4,7],[1,3,10],[0,3,11],[1,6,11],[0,4,8],[1,3,8],[3,7,10],[0,1,11],[0,7,10],[2,4,6],[2,6,10],[1,2,8],[7,8,11],[1,9,10],[0,3,4],[0,1,2],[1,8,10],[3,8,11],[1,4,11],[2,5,11],[1,3,5],[1,2,5],[2,4,9],[0,7,10],[3,5,6],[2,4,5],[0,6,9],[0,6,7],[3,4,6],[4,8,10],[4,6,11],[8,9,11],[1,8,10],[1,5,6],[0,6,7],[5,8,10],[7,9,10],[1,3,6],[0,2,4],[0,2,10],[6,7,10],[5,6,11],[7,8,9],[6,7,10],[1,3,9],[2,5,8],[2,6,10],[1,2,8],[2,6,10],[0,2,5],[0,4,9],[3,7,9],[5,8,10],[0,1,6],[1,4,10],[1,2,9],[1,8,9],[1,2,8],[0,1,2],[0,7,9],[3,7,8],[3,5,6],[0,5,8],[0,4,7],[4,7,9],[1,9,10],[3,5,6],[3,6,7],[0,5,9],[0,1,9],[1,7,10],[0,6,7],[2,7,9],[5,7,9],[2,3,6],[5,8,9],[0,2,10],[0,7,10],[0,6,10],[1,5,8],[2,7,11],[6,8,11],[3,4,8],[7,8,11],[5,10,11],[4,8,9],[3,7,10],[5,7,11],[2,4,5],[2,5,11],[2,3,5],[2,8,10],[1,2,4],[7,8,10],[1,4,10],[2,5,7],[6,8,10],[5,7,10],[2,3,5],[5,8,11],[3,6,11],[4,6,10],[1,7,11],[0,6,7],[6,9,11],[3,4,5],[3,5,10],[3,6,10],[0,1,5],[5,8,9],[0,8,10],[3,4,8],[0,1,6],[4,7,8],[2,6,7],[2,5,10],[0,5,6],[3,4,5],[1,2,10],[3,5,11],[0,3,9],[0,3,5],[5,6,10],[3,6,9],[0,1,3],[7,8,9],[5,8,11],[2,7,11],[6,10,11],[6,7,11],[0,7,11],[1,6,10],[1,7,8],[7,8,10],[4,6,10],[2,3,10],[3,4,7],[1,2,8],[5,6,9],[7,8,10],[3,4,10],[2,9,11],[7,10,11],[5,9,10],[0,6,11],[0,7,8],[0,1,10],[2,7,10],[1,2,3],[0,8,9],[5,6,10],[3,4,11],[7,9,11],[2,4,5],[1,4,6],[1,6,10],[0,2,11],[3,4,9],[2,7,9],[5,7,10],[0,3,9],[2,5,9],[2,4,11],[2,3,6],[2,4,8],[0,1,4],[3,6,8],[1,4,11],[4,7,9],[2,4,11],[1,4,8],[0,1,11],[2,4,9],[1,3,5],[0,5,9],[1,6,10],[1,4,8],[4,7,9],[0,5,8],[5,10,11],[0,1,2],[0,1,10],[2,4,11],[3,7,9],[2,3,7],[2,5,6],[1,4,6],[1,5,10],[4,8,9],[2,3,6],[0,4,10],[3,5,6],[6,8,11],[8,10,11],[2,3,6],[4,7,8],[1,6,11],[1,6,9],[2,4,11],[5,6,10],[6,10,11],[6,7,10],[4,7,11],[6,7,11],[5,6,7],[1,5,7],[4,5,10],[4,7,9],[2,6,9],[3,4,6],[4,5,9],[2,4,6],[0,5,8],[1,3,6],[0,1,6],[0,6,8],[2,5,11],[2,10,11],[0,9,11],[1,8,9],[1,2,11],[1,5,9],[1,3,6],[1,3,5],[3,7,11],[5,8,10],[1,4,6],[0,3,5],[8,9,11],[2,7,11],[0,5,7],[2,3,5],[4,9,10],[0,5,8],[3,4,10],[5,7,9],[1,2,4],[2,3,5],[2,3,9],[6,8,9],[2,7,10],[0,3,10],[3,4,11],[0,3,4],[1,5,6],[1,4,8],[2,4,10],[3,10,11],[4,7,9],[6,7,9],[1,3,9],[4,5,7],[5,8,9],[2,7,8],[2,4,8],[3,7,10],[0,6,7],[1,3,10],[0,3,7],[2,3,4],[3,4,7],[2,3,8]],[[0,9,10],[7,9,10],[0,2,6],[3,6,10],[2,5,9],[3,4,9],[2,6,10],[4,5,11],[0,7,9],[1,4,11],[4,8,10],[3,5,6],[0,4,9],[5,6,8],[2,3,8],[3,6,8],[5,6,9],[6,7,8],[0,5,6],[0,3,8],[8,9,10],[2,5,11],[1,4,8],[0,7,8],[1,5,6],[1,5,6],[3,7,11],[4,7,10],[0,3,7],[2,4,5],[1,4,6],[3,6,9],[9,10,11],[0,4,11],[7,9,11],[2,4,6],[1,4,5],[0,2,5],[2,8,9],[3,5,9],[2,7,10],[5,7,8],[0,1,5],[5,6,8],[4,5,6],[5,6,8],[0,3,9],[0,5,9],[5,7,9],[2,5,9],[3,5,6],[4,6,7],[3,4,11],[4,6,11],[4,8,11],[0,1,9],[2,5,11],[8,9,10],[1,2,6],[0,7,11],[5,7,10],[2,4,10],[1,3,7],[1,4,6],[2,4,6],[0,2,8],[0,8,10],[0,5,7],[2,4,7],[4,6,9],[4,5,8],[2,8,10],[0,6,9],[0,3,9],[4,9,10],[6,10,11],[3,6,7],[0,8,9],[1,8,10],[0,5,8],[4,7,10],[2,3,10],[2,4,5],[1,6,11],[0,1,3],[2,7,8],[2,5,10],[0,3,6],[5,10,11],[2,3,6],[1,2,4],[3,5,9],[3,4,7],[4,7,9],[0,2,3],[5,8,10],[2,5,6],[8,9,10],[4,6,7],[3,4,6],[0,3,9],[3,6,7],[0,7,11],[2,10,11],[1,2,9],[0,5,10],[1,4,5],[8,10,11],[4,7,11],[8,9,11],[7,8,10],[1,2,4],[3,5,10],[3,7,9],[0,4,6],[0,5,9],[1,2,5],[2,3,4],[3,4,11],[3,4,8],[4,7,10],[0,9,11],[0,3,8],[5,8,11],[2,4,11],[0,10,11],[2,8,10],[0,4,7],[7,10,11],[3,4,5],[3,4,7],[0,6,7],[0,4,7],[4,6,9],[0,9,10],[4,8,11],[0,4,6],[6,8,11],[3,6,11],[1,5,9],[4,5,7],[2,3,8],[2,9,11],[3,6,9],[0,5,10],[0,2,6],[0,4,11],[3,7,10],[3,6,7],[2,7,10],[2,6,7],[0,1,11],[8,9,11],[2,8,10],[0,1,5],[1,10,11],[3,6,8],[2,6,11],[2,4,9],[0,1,8],[2,8,9],[3,6,8],[5,9,11],[7,8,9],[1,4,5],[1,10,11],[1,2,9],[0,9,10],[3,9,11],[5,7,9],[1,2,5],[3,7,11],[2,4,9],[6,8,9],[2,5,9],[0,6,8],[2,7,8],[0,1,4],[0,6,8],[4,5,11],[1,6,8],[6,8,10],[0,2,6],[4,9,11],[5,7,11],[6,7,8],[0,1,6],[3,4,10],[3,6,7],[0,3,10],[0,6,10],[3,8,10],[0,5,10],[2,7,10],[0,4,11],[0,8,9],[3,8,10],[2,5,8],[3,7,8],[1,6,9],[1,9,10],[1,5,11],[5,6,8],[0,3,5],[2,6,7],[1,5,9],[0,1,4],[4,8,11],[1,4,11],[0,3,8],[3,6,7],[3,4,9],[4,8,10],[1,2,9],[3,9,11],[0,2,5],[3,5,7],[6,7,10],[4,8,9],[0,4,7],[1,8,11],[6,7,8],[0,4,9],[3,6,7],[1,4,7],[0,5,6],[5,7,9],[4,6,9],[1,5,7],[1,7,10],[1,6,8],[0,4,11],[1,4,11],[5,9,11],[5,9,11],[2,3,6],[2,4,8],[2,6,11],[2,4,8],[4,7,10],[1,8,9],[1,5,7],[8,9,10],[0,3,10],[3,6,8],[4,10,11],[5,9,10],[3,4,7],[0,1,10],[4,7,8],[3,7,8],[6,10,11],[5,6,9],[1,2,11],[2,5,8],[1,3,9],[6,8,9],[1,4,9],[2,3,5],[4,5,8],[5,9,10],[2,7,9],[4,9,10],[0,2,7],[4,5,9],[1,7,8],[3,7,11],[0,8,10],[2,6,8],[0,4,7],[1,10,11],[2,5,7],[3,7,9],[2,8,11],[1,5,6],[2,5,10],[2,9,10],[6,9,11],[0,7,11],[7,8,10],[2,6,10],[1,5,8],[2,3,9],[0,5,11],[4,8,11],[2,3,8],[1,4,10],[5,6,10],[3,4,8],[1,2,6],[0,2,5],[0,2,11],[4,5,7],[4,6,7],[3,9,10],[1,3,9],[1,4,11],[1,9,10],[3,7,9],[6,9,11],[2,6,11],[0,2,11],[2,3,10],[1,6,7],[0,4,7],[2,8,10],[0,6,9],[1,2,3],[2,5,8],[1,5,9],[5,8,10],[0,2,7],[0,3,8],[5,6,9],[1,5,8],[0,1,4],[0,8,9],[0,5,10],[2,4,5],[0,7,8],[5,6,8],[6,10,11],[1,7,11],[4,9,11],[0,4,7],[1,7,9],[0,7,10],[1,2,7],[0,6,11],[7,10,11],[5,9,11],[1,4,6],[2,7,10],[1,2,4],[5,6,10],[6,7,9],[4,5,8],[5,8,11],[0,4,9],[0,1,8],[3,5,9],[1,2,8],[1,4,10],[0,6,7],[0,7,8],[5,7,11],[3,7,9],[1,5,7],[1,3,5],[2,5,6],[4,7,10],[0,3,7],[1,4,10],[0,2,7],[2,7,10],[0,5,6],[1,2,11],[2,7,10],[4,7,8],[0,5,9],[1,3,7],[6,7,8],[2,7,11],[2,6,9],[2,10,11],[0,7,9],[1,9,10],[0,1,7],[5,6,9],[5,7,8],[5,9,10],[0,4,10],[1,2,4],[6,8,10],[1,3,11],[2,4,5],[4,6,9],[0,6,9],[2,5,7],[3,5,11],[7,8,9],[0,3,11],[8,9,11],[4,5,9],[5,9,10],[0,10,11],[0,8,9],[0,2,6],[1,4,5],[4,7,10],[1,4,11],[4,8,9],[0,2,3],[3,4,10],[4,9,10],[3,7,9],[3,8,10],[2,9,10],[2,7,9],[1,3,7],[4,9,10],[6,8,11],[2,7,11],[1,8,10],[2,4,7],[3,6,9],[1,4,9],[3,4,9],[3,4,6],[1,9,10],[1,4,6],[0,1,8],[2,6,7],[1,6,8],[1,2,7],[2,5,7],[7,8,11],[0,2,3],[0,2,5],[2,5,11],[4,5,6],[3,5,9],[2,6,9],[1,5,7],[3,5,10],[1,6,9],[2,4,6],[0,4,5],[8,9,10],[2,6,7],[0,3,4],[4,5,10],[3,5,8],[0,2,5],[2,10,11],[1,2,3],[6,10,11],[1,2,10],[7,8,10],[4,5,8],[1,6,9],[1,5,7],[0,6,7],[0,2,4],[1,2,7],[0,3,5],[3,4,5],[0,6,10],[1,3,10],[3,7,10],[3,9,11],[0,3,6],[2,6,10],[2,3,4],[1,6,11],[1,8,11],[6,8,10],[1,6,10],[3,4,6],[0,8,9],[0,4,7],[5,6,7],[0,10,11],[5,8,9],[8,10,11],[2,4,11],[0,1,2],[1,8,10],[1,4,7],[1,3,9],[2,9,10],[0,8,10],[3,7,8],[2,6,9],[0,1,2],[0,3,11],[3,10,11],[4,6,9],[2,9,10],[0,9,10],[2,3,8],[1,7,10],[0,2,3],[5,7,8],[5,8,10],[0,1,6],[3,5,7],[0,6,8],[0,1,2],[9,10,11],[0,3,7],[1,8,9],[3,4,9],[0,1,8],[8,9,10],[4,6,9],[0,1,9],[3,6,8],[3,8,9],[5,10,11],[1,2,9],[0,3,10],[0,8,9],[4,8,11],[0,6,10],[3,5,9],[5,6,8],[1,3,10],[2,6,7],[2,6,11],[1,9,10],[6,9,11]],[[5,7,10],[0,4,10],[1,3,9],[2,6,7],[2,3,9],[2,4,6],[9,10,11],[2,3,6],[3,6,10],[0,7,11],[0,5,7],[5,9,10],[2,3,11],[0,3,11],[4,5,9],[0,6,9],[0,2,6],[0,6,9],[5,8,9],[2,5,11],[1,4,10],[2,3,7],[6,8,10],[1,3,8],[1,5,7],[4,8,9],[1,3,4],[5,9,10],[2,3,11],[1,3,8],[6,9,10],[4,9,10],[1,3,6],[3,10,11],[0,7,11],[0,10,11],[4,5,8],[0,2,5],[1,6,7],[1,6,8],[1,6,7],[4,7,10],[0,2,8],[0,3,6],[0,1,3],[6,9,11],[7,9,10],[0,7,8],[5,8,10],[0,5,9],[7,8,11],[4,7,11],[3,5,6],[1,5,11],[5,8,9],[2,3,9],[0,2,8],[3,6,9],[5,6,10],[5,8,10],[3,5,11],[1,4,5],[2,9,11],[0,2,5],[3,6,8],[2,5,8],[1,7,8],[9,10,11],[5,8,11],[6,8,9],[3,7,10],[0,3,5],[1,7,9],[0,3,5],[0,7,8],[1,4,8],[8,9,11],[0,2,11],[2,3,8],[3,10,11],[1,2,4],[2,7,8],[1,6,10],[2,8,10],[3,8,10],[3,5,9],[5,6,7],[3,5,7],[1,9,11],[1,5,8],[1,4,10],[2,4,6],[0,6,9],[1,3,5],[0,3,10],[0,1,5],[0,6,11],[2,7,9],[0,2,6],[4,6,7],[3,6,10],[8,9,10],[7,8,11],[0,10,11],[8,10,11],[1,10,11],[0,1,3],[3,9,10],[1,9,10],[1,5,8],[3,7,8],[0,3,4],[4,5,10],[3,5,11],[1,4,7],[1,9,11],[3,9,11],[6,9,10],[5,8,11],[5,7,8],[2,7,9],[2,3,10],[5,6,7],[3,10,11],[0,3,6],[1,10,11],[0,7,9],[6,8,11],[2,5,10],[9,10,11],[2,3,8],[0,1,2],[6,7,8],[1,2,11],[3,5,9],[0,2,8],[1,3,5],[2,6,7],[3,7,10],[3,7,10],[2,3,7],[3,5,8],[4,7,11],[2,3,4],[8,9,10],[1,5,10],[1,2,3],[7,9,10],[0,7,10],[8,9,10],[2,3,4],[6,9,10],[1,9,11],[3,5,10],[3,7,11],[4,6,10],[6,10,11],[9,10,11],[6,7,10],[0,4,9],[1,4,8],[0,6,10],[4,9,10],[0,1,11],[2,9,10],[1,3,11],[3,7,10],[1,2,9],[4,5,6],[1,4,8],[0,2,5],[0,8,9],[0,7,11],[0,1,3],[3,4,11],[6,8,9],[4,7,9],[0,3,10],[0,1,5],[1,3,5],[2,7,10],[3,8,10],[2,7,11],[0,2,5],[8,10,11],[1,7,8],[0,4,7],[3,6,10],[0,3,9],[4,5,10],[0,6,10],[5,7,8],[0,3,5],[0,2,11],[3,4,9],[4,7,11],[0,1,3],[4,9,11],[0,2,3],[4,8,11],[0,3,9],[0,6,8],[0,1,6],[1,6,10],[2,3,11],[8,10,11],[0,7,11],[3,5,9],[2,3,8],[0,7,8],[2,6,7],[0,5,9],[1,4,7],[2,3,6],[0,1,11],[1,2,7],[7,9,10],[4,7,11],[2,3,11],[1,9,11],[1,2,10],[1,4,8],[4,8,9],[0,4,5],[4,9,10],[1,2,5],[7,10,11],[1,6,8],[4,7,8],[0,2,8],[1,8,11],[1,3,8],[0,3,11],[0,1,7],[0,7,9],[1,4,8],[2,3,6],[1,2,7],[1,5,10],[2,7,10],[4,5,7],[0,5,7],[3,7,9],[2,4,8],[2,3,5],[5,7,9],[3,6,7],[4,8,11],[0,4,7],[3,5,8],[0,5,11],[4,6,11],[3,8,10],[0,1,5],[2,5,9],[1,3,6],[0,10,11],[0,4,9],[0,1,6],[0,7,11],[1,2,8],[9,10,11],[1,6,10],[0,9,10],[0,10,11],[0,5,7],[0,1,4],[0,1,11],[2,4,10],[2,4,8],[0,2,11],[4,7,10],[2,5,8],[5,9,11],[1,2,8],[3,7,9],[2,7,9],[6,8,9],[0,5,7],[1,4,7],[3,7,11],[3,4,5],[3,7,9],[2,8,10],[0,8,9],[5,8,10],[1,3,8],[1,7,8],[8,9,11],[3,6,11],[0,2,5],[1,3,7],[3,5,11],[3,8,11],[1,2,11],[1,6,7],[4,5,7],[0,2,9],[9,10,11],[0,2,8],[2,4,10],[0,7,9],[7,9,11],[0,7,11],[4,9,11],[2,6,10],[0,2,6],[1,4,6],[2,8,10],[4,6,11],[7,10,11],[2,7,9],[2,5,7],[1,5,7],[2,9,11],[2,8,9],[2,7,10],[6,8,10],[0,4,7],[2,4,10],[0,2,9],[0,2,8],[3,6,10],[2,3,5],[0,4,8],[3,10,11],[1,7,8],[1,2,5],[4,9,10],[4,7,8],[2,6,11],[0,9,10],[1,2,8],[1,4,9],[0,8,9],[3,5,8],[0,3,8],[2,7,11],[1,6,10],[0,2,8],[3,4,7],[6,9,11],[0,4,10],[2,5,7],[3,6,9],[2,4,5],[1,4,11],[0,8,10],[3,6,9],[0,10,11],[5,6,7],[0,5,6],[2,8,9],[3,8,9],[0,3,5],[3,5,9],[4,9,10],[2,3,10],[1,9,10],[4,7,11],[4,6,7],[4,9,11],[5,6,8],[4,6,8],[0,1,2],[3,6,7],[3,9,10],[1,7,9],[4,5,11],[1,7,9],[3,9,11],[2,4,10],[1,7,10],[2,5,7],[1,3,7],[2,8,11],[3,7,8],[2,4,10],[1,7,9],[3,4,8],[0,8,9],[1,3,11],[4,6,7],[4,10,11],[0,4,10],[0,4,8],[1,10,11],[0,1,8],[4,7,11],[3,8,10],[2,8,10],[0,4,10],[4,8,10],[3,5,10],[1,4,11],[4,6,8],[0,1,8],[5,6,11],[1,5,9],[3,8,11],[1,5,7],[4,5,11],[0,6,11],[3,4,7],[4,5,10],[0,4,10],[3,9,10],[1,2,3],[7,8,9],[5,7,8],[3,4,8],[6,10,11],[0,10,11],[2,6,11],[2,8,9],[2,5,7],[1,4,10],[4,8,9],[2,7,10],[3,10,11],[1,7,10],[4,5,6],[2,3,10],[1,4,8],[1,4,9],[2,6,11],[0,1,9],[2,4,9],[0,1,6],[7,9,10],[4,6,11],[1,10,11],[0,5,7],[0,5,6],[1,3,10],[0,5,9],[0,2,8],[6,8,10],[4,6,11],[0,7,8],[0,2,5],[0,7,9],[2,9,11],[3,4,8],[1,4,7],[3,7,8],[0,2,11],[2,7,10],[0,4,8],[3,6,9],[1,3,5],[0,1,5],[1,3,4],[0,5,6],[1,7,9],[0,6,11],[4,7,11],[4,8,10],[2,5,9],[1,9,10],[3,7,8],[5,9,11],[0,5,10],[6,8,10],[3,4,8],[2,3,7],[4,8,9],[7,9,10],[2,4,8],[0,2,10],[1,6,8],[4,6,11],[1,3,4],[1,2,6],[4,5,11],[4,5,9],[0,3,6],[5,9,11],[4,5,9],[2,5,7],[2,9,11],[4,5,8],[1,3,8],[0,3,7],[0,2,5],[1,2,5],[1,8,11],[2,4,9],[2,3,4],[5,6,10],[0,4,11],[0,4,9],[2,7,11],[1,9,11],[2,3,9],[0,1,8],[4,6,11],[2,6,7],[1,2,3],[1,6,9],[1,2,5],[3,10,11],[0,9,10],[3,7,9],[0,1,8],[1,5,9],[4,5,9],[2,5,8],[1,4,11],[0,1,7],[6,7,9],[7,8,11]],[[0,6,10],[0,2,10],[3,7,9],[2,5,9],[2,4,6],[2,8,11],[1,6,8],[3,7,11],[5,7,9],[6,9,11],[0,8,9],[0,3,5],[4,9,10],[0,9,10],[2,8,9],[0,5,11],[0,5,7],[7,9,11],[0,6,9],[3,5,11],[0,5,10],[1,3,6],[2,6,9],[2,6,9],[3,6,10],[2,6,7],[3,5,11],[1,2,8],[2,5,11],[7,9,11],[5,7,9],[4,6,7],[2,8,10],[4,5,11],[2,6,9],[8,10,11],[1,3,5],[0,3,10],[4,6,8],[3,6,8],[0,6,11],[4,9,11],[3,4,9],[6,7,10],[0,1,7],[0,1,3],[1,2,3],[5,6,10],[1,9,10],[1,8,11],[2,7,9],[1,3,8],[0,1,9],[0,8,11],[1,2,6],[1,6,8],[2,3,9],[5,6,11],[1,3,4],[4,8,9],[1,2,6],[0,4,8],[7,9,11],[2,7,8],[5,7,11],[1,4,5],[4,6,9],[3,8,10],[4,5,11],[0,1,8],[4,8,11],[1,2,11],[3,4,8],[1,3,7],[3,7,10],[2,6,9],[5,6,9],[2,10,11],[1,2,7],[2,6,7],[1,10,11],[3,4,9],[3,6,11],[0,2,10],[4,9,10],[5,6,11],[3,5,9],[1,10,11],[1,8,10],[6,7,11],[4,9,11],[2,6,8],[4,8,9],[2,4,5],[4,7,11],[3,6,9],[0,4,6],[1,3,8],[0,2,7],[6,8,11],[2,9,11],[8,9,10],[1,4,10],[4,9,10],[1,5,10],[4,5,7],[0,1,4],[6,8,11],[6,7,9],[4,5,6],[3,4,9],[0,4,10],[4,5,11],[3,5,11],[3,4,5],[5,6,11],[2,8,10],[3,5,9],[0,2,6],[0,1,9],[0,2,5],[2,3,5],[4,5,7],[0,7,10],[7,9,10],[0,1,9],[1,3,5],[5,8,10],[5,6,9],[1,4,9],[1,7,10],[0,2,7],[3,4,7],[2,6,8],[6,9,11],[3,5,11],[0,5,10],[5,6,11],[1,8,9],[2,3,10],[5,7,9],[6,10,11],[0,3,5],[1,8,11],[1,3,7],[0,6,7],[1,3,6],[3,8,11],[3,10,11],[4,7,9],[3,6,9],[0,1,6],[1,8,9],[3,6,7],[0,1,8],[1,3,8],[2,3,9],[6,7,10],[0,4,8],[0,2,10],[0,5,9],[0,4,10],[1,2,9],[1,5,11],[1,6,8],[0,7,10],[7,8,11],[0,8,11],[1,3,9],[3,6,11],[4,8,10],[0,6,11],[3,8,11],[2,3,11],[1,4,8],[0,3,11],[3,4,8],[3,5,10],[1,2,6],[2,5,6],[0,6,7],[3,5,6],[2,5,6],[2,3,9],[2,3,11],[2,6,11],[0,2,10],[0,3,6],[1,3,8],[6,7,9],[2,3,8],[1,9,11],[0,7,11],[5,7,9],[0,9,10],[2,3,11],[1,8,9],[2,3,7],[2,4,8],[4,5,6],[3,5,8],[1,2,7],[1,3,6],[1,5,7],[1,5,6],[0,6,9],[1,2,11],[1,2,4],[1,6,7],[2,3,11],[0,8,10],[0,5,9],[0,3,5],[5,7,9],[0,8,9],[0,3,8],[0,10,11],[1,2,7],[2,3,11],[1,2,4],[1,9,10],[1,2,11],[5,8,9],[1,4,5],[2,3,4],[4,5,6],[0,6,8],[1,2,10],[1,9,11],[4,10,11],[0,7,11],[1,2,4],[0,1,11],[4,5,11],[0,3,11],[2,8,9],[6,10,11],[0,8,11],[3,4,6],[1,3,11],[0,6,8],[1,2,8],[1,3,10],[1,4,10],[3,7,11],[1,5,6],[1,2,11],[0,6,10],[2,5,9],[0,3,7],[0,1,8],[3,8,11],[0,9,10],[0,2,8],[5,8,11],[1,5,6],[3,6,7],[3,5,11],[0,9,10],[1,6,8],[8,10,11],[3,4,5],[1,7,8],[4,5,11],[5,9,10],[1,8,10],[9,10,11],[2,10,11],[0,5,7],[4,5,10],[1,5,8],[0,3,7],[0,6,8],[3,4,8],[0,3,9],[2,4,11],[4,6,10],[3,6,10],[3,5,11],[2,4,9],[2,5,11],[0,8,11],[3,7,9],[1,6,10],[7,8,11],[4,6,8],[2,9,10],[1,4,7],[2,5,8],[6,7,9],[9,10,11],[0,2,8],[5,6,8],[3,4,5],[1,6,11],[2,10,11],[3,8,10],[1,5,8],[2,3,8],[0,2,7],[3,4,5],[3,4,9],[1,4,5],[0,3,9],[2,9,11],[0,10,11],[0,2,3],[2,6,10],[4,7,11],[4,5,6],[2,7,9],[4,6,8],[2,6,9],[1,2,6],[1,6,7],[0,1,3],[6,7,10],[1,2,11],[2,3,10],[5,6,8],[2,5,11],[6,7,8],[0,4,5],[0,1,10],[5,8,9],[7,10,11],[1,4,9],[2,5,11],[1,5,6],[1,3,5],[5,6,11],[2,7,11],[5,10,11],[1,4,9],[6,8,10],[0,2,8],[2,8,9],[2,6,9],[1,5,7],[5,7,10],[3,8,9],[1,3,10],[1,5,11],[1,2,8],[0,5,10],[5,7,9],[2,5,6],[0,6,9],[3,6,8],[1,3,11],[4,7,9],[3,4,9],[3,6,10],[7,8,9],[3,5,9],[0,1,6],[3,5,10],[3,8,11],[5,9,11],[0,5,11],[2,5,8],[0,3,10],[2,5,8],[2,7,10],[3,6,8],[6,7,11],[2,4,7],[1,3,6],[2,5,9],[2,4,7],[4,6,8],[0,8,11],[2,5,8],[3,6,8],[5,7,11],[1,2,10],[1,2,4],[0,1,10],[0,7,8],[8,9,11],[4,7,10],[2,9,11],[4,5,8],[0,2,8],[6,7,8],[3,5,8],[2,7,9],[6,7,11],[6,8,11],[1,6,8],[0,1,4],[0,8,9],[3,6,7],[0,6,10],[3,5,11],[1,4,11],[5,6,8],[1,3,7],[6,7,8],[3,7,8],[3,7,11],[0,6,7],[4,9,11],[0,3,8],[5,7,10],[5,9,10],[3,5,10],[1,9,10],[2,3,6],[0,1,6],[2,8,10],[0,1,4],[0,4,6],[7,9,11],[2,7,8],[1,3,7],[2,3,6],[2,5,8],[3,10,11],[6,8,9],[0,8,11],[0,2,3],[0,1,3],[1,3,7],[2,10,11],[2,6,8],[6,9,10],[8,9,10],[1,4,8],[1,2,5],[0,3,9],[3,8,10],[2,5,9],[1,9,11],[1,7,11],[2,4,6],[2,3,6],[5,7,11],[1,7,11],[7,9,10],[1,4,10],[3,8,9],[0,5,9],[0,3,9],[3,7,9],[0,2,6],[5,7,8],[1,6,11],[4,5,9],[1,2,6],[0,2,5],[2,3,7],[0,5,7],[0,2,4],[0,3,7],[3,5,7],[0,5,6],[0,2,3],[2,5,7],[2,5,7],[2,8,11],[0,6,9],[8,9,11],[0,4,11],[2,4,7],[1,8,11],[2,5,8],[3,7,11],[5,6,11],[2,7,10],[2,3,9],[0,1,10],[3,6,8],[2,3,10],[1,4,10],[0,4,8],[0,2,4],[2,4,9],[0,6,9],[3,5,11],[7,9,10],[0,1,9],[0,7,10],[0,2,11],[0,2,5],[3,8,11],[5,7,11],[1,5,7],[2,4,6],[2,4,11],[6,7,10],[2,8,9],[0,3,8],[1,5,11],[0,3,6],[0,6,7],[4,10,11],[0,8,11],[4,7,8],[1,8,10],[0,2,6],[8,9,10],[4,5,6],[5,8,10],[1,2,9],[8,9,10],[9,10,11],[3,6,10],[4,5,7],[2,6,10],[8,10,11],[3,6,11]],[[2,3,5],[1,4,10],[0,3,11],[5,10,11],[1,5,8],[0,5,11],[2,7,10],[0,7,10],[1,4,9],[4,6,9],[2,5,11],[0,1,3],[1,5,11],[1,3,4],[1,9,10],[2,6,7],[0,3,5],[0,6,8],[2,5,11],[2,3,9],[4,7,8],[5,10,11],[0,4,11],[0,10,11],[4,7,10],[2,7,9],[1,2,10],[4,7,8],[1,9,11],[1,2,7],[0,1,4],[1,7,9],[1,3,9],[2,3,5],[2,5,7],[4,5,8],[3,7,10],[1,4,8],[1,4,5],[0,5,10],[0,2,3],[0,3,8],[4,8,11],[1,6,8],[3,4,6],[3,6,7],[3,7,9],[1,2,5],[2,8,11],[1,3,10],[5,7,11],[2,4,6],[2,3,7],[3,5,11],[2,8,10],[2,8,10],[2,5,6],[1,4,6],[4,5,9],[1,7,8],[7,10,11],[1,3,6],[0,3,8],[3,9,11],[1,7,10],[3,5,6],[0,2,5],[5,8,10],[0,7,8],[2,7,8],[0,5,6],[0,1,5],[5,7,10],[0,1,3],[2,6,9],[0,5,11],[1,4,7],[2,4,7],[0,3,10],[2,3,7],[1,2,10],[4,7,8],[2,5,9],[2,5,8],[0,4,11],[0,5,11],[1,4,10],[4,5,7],[2,3,10],[1,2,3],[7,8,9],[0,2,3],[1,5,8],[2,4,6],[1,2,7],[5,6,10],[2,8,11],[5,9,11],[0,5,8],[4,7,11],[7,10,11],[0,5,8],[4,8,9],[5,7,8],[4,7,10],[2,4,6],[8,9,10],[0,2,5],[3,4,5],[4,6,11],[1,2,9],[0,8,11],[0,5,9],[5,7,9],[3,4,6],[0,5,9],[5,6,8],[3,5,9],[8,9,10],[1,4,10],[1,5,9],[1,8,10],[1,6,10],[4,6,8],[2,5,11],[1,5,7],[1,3,11],[1,3,6],[2,8,11],[0,6,8],[2,7,9],[0,3,6],[2,10,11],[9,10,11],[7,9,10],[2,6,7],[3,8,10],[2,6,10],[4,5,7],[0,5,11],[3,4,7],[3,10,11],[0,7,10],[4,5,6],[2,10,11],[2,4,6],[3,7,8],[2,3,7],[5,6,7],[3,5,7],[0,2,9],[2,9,10],[1,7,9],[6,9,11],[1,3,8],[3,4,9],[3,5,9],[1,2,11],[0,1,2],[1,5,9],[0,2,5],[2,3,6],[1,4,11],[3,6,7],[2,6,11],[5,6,7],[3,7,10],[2,5,9],[6,8,11],[1,2,11],[0,3,11],[3,5,9],[2,4,11],[3,5,6],[1,4,5],[4,5,8],[2,10,11],[0,6,7],[2,7,8],[3,4,5],[2,3,8],[0,7,8],[1,3,8],[2,4,9],[1,2,3],[0,6,7],[2,3,5],[2,6,7],[0,9,11],[5,6,10],[5,10,11],[1,3,5],[2,7,9],[4,7,11],[1,6,9],[1,6,8],[3,7,8],[2,4,8],[2,3,8],[5,8,11],[2,5,9],[3,5,11],[4,8,11],[1,3,8],[1,3,7],[1,4,11],[5,6,9],[6,8,9],[0,7,9],[0,4,6],[0,2,8],[0,6,7],[2,9,10],[0,2,10],[4,5,10],[5,7,8],[6,8,10],[2,6,9],[1,2,8],[5,7,11],[1,4,9],[1,9,10],[4,6,11],[6,8,11],[1,2,8],[6,7,8],[0,3,7],[5,10,11],[2,4,7],[3,7,9],[3,6,10],[5,7,11],[5,6,8],[4,10,11],[3,4,11],[7,10,11],[0,4,9],[0,7,8],[3,5,8],[3,6,8],[0,2,3],[1,2,5],[2,3,8],[0,2,9],[4,6,7],[0,1,2],[0,2,7],[5,7,9],[0,7,11],[0,6,10],[7,8,11],[0,2,6],[3,9,10],[2,3,8],[9,10,11],[3,5,6],[6,8,9],[0,1,2],[2,9,11],[4,10,11],[5,6,7],[1,8,10],[3,5,8],[2,3,9],[0,9,10],[1,7,11],[2,4,5],[4,6,10],[4,7,8],[0,4,10],[2,3,6],[5,8,10],[1,2,3],[1,3,11],[2,5,6],[1,4,10],[0,4,11],[0,4,9],[2,7,9],[0,3,4],[0,5,7],[5,7,8],[5,6,11],[2,5,9],[7,9,11],[1,2,6],[1,3,9],[6,8,9],[3,5,7],[5,9,10],[1,9,11],[1,6,11],[7,9,10],[5,6,7],[3,6,11],[1,3,5],[3,7,8],[0,5,10],[0,8,9],[0,6,7],[4,5,7],[0,1,3],[1,4,5],[3,4,9],[3,6,10],[1,6,8],[4,5,8],[2,3,10],[0,1,6],[0,2,8],[4,7,8],[2,7,11],[5,6,10],[4,8,10],[0,2,4],[0,6,11],[4,7,8],[1,8,10],[0,4,8],[3,6,8],[1,5,8],[6,8,10],[4,8,10],[3,5,9],[4,5,8],[1,4,8],[3,10,11],[0,1,4],[0,6,7],[1,8,9],[2,7,11],[1,5,11],[3,8,9],[0,4,8],[0,3,4],[0,3,4],[4,5,8],[2,6,9],[0,3,8],[2,7,11],[3,8,11],[5,8,11],[0,1,3],[2,6,10],[2,5,6],[6,8,10],[1,5,10],[6,9,11],[1,8,11],[3,4,7],[1,5,8],[0,3,6],[0,3,10],[0,1,6],[2,7,8],[1,6,8],[0,5,8],[2,6,10],[0,4,10],[0,4,5],[7,9,10],[6,8,10],[6,7,8],[0,1,10],[3,9,11],[0,4,11],[0,5,8],[0,4,11],[8,9,11],[4,5,9],[3,6,8],[1,2,11],[6,9,11],[1,4,5],[1,2,9],[4,7,11],[1,2,5],[7,10,11],[0,6,11],[2,4,11],[3,8,9],[7,10,11],[0,1,2],[1,7,10],[7,8,11],[1,6,8],[4,9,10],[0,3,10],[2,3,10],[8,9,11],[1,5,11],[4,6,9],[2,3,6],[4,6,8],[3,8,11],[0,2,7],[0,1,10],[2,4,7],[3,5,11],[4,8,9],[0,2,4],[2,8,10],[1,5,6],[2,3,6],[3,8,10],[5,9,10],[6,9,10],[0,2,5],[0,4,7],[1,3,9],[2,3,5],[1,2,11],[4,7,10],[2,4,10],[0,1,10],[2,7,11],[0,2,9],[0,1,4],[5,8,11],[0,2,9],[2,3,8],[0,6,7],[1,6,7],[7,8,11],[0,1,5],[0,6,11],[3,5,9],[4,5,10],[2,4,9],[3,9,11],[0,2,9],[1,2,11],[1,7,8],[8,10,11],[0,9,10],[5,7,9],[1,3,5],[1,7,10],[2,4,5],[5,7,8],[7,8,10],[3,10,11],[3,5,9],[1,7,10],[5,8,9],[3,6,10],[5,6,11],[1,4,11],[0,1,11],[2,3,5],[1,5,7],[5,7,10],[3,5,7],[4,8,10],[0,1,11],[2,4,10],[3,4,11],[1,4,11],[1,4,6],[5,6,11],[5,7,8],[0,5,6],[2,5,11],[6,7,10],[6,10,11],[3,8,11],[6,8,11],[5,7,8],[3,6,10],[6,7,11],[3,7,8],[2,3,10],[5,7,11],[1,8,10],[2,9,11],[0,3,10],[2,5,7],[5,7,9],[3,5,7],[5,10,11],[1,3,11],[5,9,11],[3,6,11],[1,6,9],[3,6,8],[1,5,10],[1,4,9],[0,8,11],[3,8,11],[1,6,9],[4,6,9],[3,4,6],[6,8,11],[4,7,11],[2,9,11],[1,2,3],[1,7,8],[1,2,3],[1,3,11],[1,5,8],[0,7,8],[1,2,10],[1,4,10],[4,5,9],[0,5,11],[6,8,9],[4,5,10],[3,7,9],[1,2,7],[3,5,9],[5,7,11],[4,6,8]]]
def setup_inputs(rng):
    return {"x": rng.standard_normal((N, 128, TOK), dtype=np.float32).astype(ml_dtypes.bfloat16), "gate": (0.5 * rng.integers(1, 4, size=(N, K, TOK)) * (2 * rng.integers(0, 2, size=(N, K, TOK)) - 1)).astype(np.float32).astype(ml_dtypes.bfloat16), "w1": (rng.standard_normal((N, 128, FT * 128), dtype=np.float32) / 8).astype(ml_dtypes.bfloat16), "w2": (rng.standard_normal((N, 128, FT * 128), dtype=np.float32) / 8).astype(ml_dtypes.bfloat16)}
def setup_inputs_big(rng):
    d = setup_inputs(rng)
    for k in ("x", "gate", "w1", "w2"): d[k] = (d[k].astype(np.float32) * 1024.0).astype(d[k].dtype)
    return d
def setup_inputs_small(rng):
    d = setup_inputs(rng)
    for k in ("x", "gate", "w1", "w2"): d[k] = (d[k].astype(np.float32) * (1 / 1024.0)).astype(d[k].dtype)
    return d
def reference(x, gate, w1, w2):
    X, GATE, W1, W2 = x.astype(np.float64), gate.astype(np.float64), w1.astype(np.float64), w2.astype(np.float64)
    y = np.zeros((N, 128, TOK))
    for r in range(N):
        for t in range(TOK):
            for i, e in enumerate(ROUTE[r][t]):
                hid = np.maximum(W1[e].T @ X[r][:, t], 0.0)
                y[r][:, t] += GATE[r][i, t] * sum(W2[e][:, 128 * f:128 * f + 128].T @ hid[128 * f:128 * f + 128] for f in range(FT))
    return {"y": y.astype(ml_dtypes.bfloat16)}

@@ -1,0 +1,264 @@
+from concourse.bass import DstId, RemoteDMATransfer
+from concourse.mybir import AluOpType
+
+NR = 12
+D = 128
+TOKN = 512
+WB = 2 * D
+NH = 2
+CW = TOKN // NH
+NU = NR * NH
+WIN = 12
+SECS = {}
+for _d2 in range(2, NR):
+    for _d1 in range(1, _d2):
+        SECS[(_d1, _d2)] = len(SECS)
+TABL = 688
+
+SCRATCH = {
+    "wall": ("sbuf", [128, NR * WB], "bfloat16"),
+    "xsb": ("sbuf", [128, TOKN], "bfloat16"),
+    "gsb": ("sbuf", [128, TOKN], "bfloat16"),
+    "tab": ("sbuf", [128, TABL], "bfloat16"),
+    "zero": ("sbuf", [128, TOKN], "bfloat16"),
+    "ones": ("sbuf", [128, D], "bfloat16"),
+    "ed": ("dram", [NR, NR + 1, D], "bfloat16"),
+    "esb": ("sbuf", [128, NR * D], "bfloat16"),
+    "gs": ("sbuf", [128, TOKN], "bfloat16"),
+    "h0": ("sbuf", [128, CW], "bfloat16"),
+    "h1": ("sbuf", [128, CW], "bfloat16"),
+    "hs": ("sbuf", [128, NU * CW], "bfloat16"),
+    "ysb": ("sbuf", [128, TOKN], "bfloat16"),
+    "zb0": ("psum", [128, 512], "float32"),
+    "zb1": ("psum", [128, 512], "float32"),
+    "gb0": ("psum", [128, 512], "float32"),
+    "gb1": ("psum", [128, 512], "float32"),
+    "ya0": ("psum", [128, 512], "float32"),
+    "ya1": ("psum", [128, 512], "float32"),
+    "gps": ("psum", [128, 512], "float32"),
+}
+SEMAPHORES = (["arr%d" % s for s in range(NR)]
+              + ["%s%d" % (n, u) for n in ("z", "gb", "rl", "hs") for u in range(NU)]
+              + ["%s%d" % (n, c) for n in ("yc", "cp", "st") for c in range(NH)]
+              + ["ldw", "ldx", "ldg", "gz", "on", "zr", "tz", "tb", "gg", "gcp", "edw", "esr", "snd"])
+
+_CACHE = {}
+
+
+def _bits(m):
+    return [i for i in range(m.bit_length()) if (m >> i) & 1]
+
+
+def _mask(engs):
+    m = 0
+    for e in engs:
+        m |= 1 << e
+    return m
+
+
+def _plan(T, topo):
+    if "p" in _CACHE:
+        return _CACHE["p"]
+    cores = list(T.cores)
+    nworld = topo.CORES_PER_HOST * (max(topo.host(c) for c in cores) + 1)
+
+    def linked(a, b):
+        return any(topo.may_write(u, v) for u in cores if topo.host(u) == a for v in cores if topo.host(v) == b and u != v)
+
+    def relay(S, same_die):
+        for k in range(nworld):
+            if k in cores or topo.host(k) != topo.host(S) or topo.chip(k) != topo.chip(S):
+                continue
+            if (topo.die(k) == topo.die(S)) != same_die:
+                continue
+            if all(topo.may_write(k, d) for d in cores if linked(topo.host(k), topo.host(d))):
+                return k
+        return None
+
+    P = [relay(S, False) for S in cores]
+    Q = [relay(S, True) for S in cores]
+    twin = []
+    for S in cores:
+        twin.append([t for t, X in enumerate(cores) if topo.rack(topo.host(X)) != topo.rack(topo.host(S))
+                     and topo.chip(X) == topo.chip(S) and topo.may_write(S, X)][0])
+    calls, cnt, klass = {}, {}, {}
+    second = []
+    for s, S in enumerate(cores):
+        tw = twin[s]
+        direct, viaP, viaQ, farP, farQ = [], [], [], [], []
+        for d, X in enumerate(cores):
+            if d == s:
+                klass[(d, s)] = 0
+            elif topo.rack(topo.host(X)) == topo.rack(topo.host(S)):
+                if topo.may_write(S, X):
+                    direct.append(X)
+                    klass[(d, s)] = 1
+                else:
+                    (viaP if topo.host(X) == topo.host(S) else viaQ).append(X)
+                    klass[(d, s)] = 2
+            elif topo.host(X) == topo.host(cores[tw]):
+                farQ.append(X)
+                klass[(d, s)] = 3
+            else:
+                farP.append(X)
+                klass[(d, s)] = 4
+        off = _bits(topo.mask(S, P[tw]))
+        onl = [e for e in _bits(topo.mask(S, P[s])) if e not in off]
+        first = [([P[tw], Q[tw]], off[0::2]), (direct, off[1::2]),
+                 ([k for k, lst in ((P[s], viaP), (Q[s], viaQ)) if lst], onl)]
+        calls[S] = [(s, [(ds, en) for ds, en in first if ds])]
+        for k, lst in ((P[s], viaP), (Q[s], viaQ)):
+            if lst:
+                calls.setdefault(k, []).append((s, [(lst, _bits(topo.mask(k, lst[0])))]))
+        for k, lst in ((P[tw], farP), (Q[tw], farQ)):
+            second.append((k, (s, [(lst, [e for e in _bits(topo.mask(k, lst[0])) if all((topo.mask(k, x) >> e) & 1 for x in lst)])])))
+    for k, c in second:
+        calls.setdefault(k, []).append(c)
+    for k, lst in calls.items():
+        for s, trs in lst:
+            for ds, en in trs:
+                for x in ds:
+                    cnt[(x, s)] = len(en)
+    order = [sorted(range(len(cores)), key=lambda s: (klass[(d, s)], s)) for d in range(len(cores))]
+    _CACHE["p"] = (calls, cnt, order)
+    return _CACHE["p"]
+
+
+def _send(g, core, T, topo, calls, cnt, own):
+    total = 0
+    for s, trs in calls:
+        if s == own:
+            g.wait_ge(T.sem.ldw, 32)
+        else:
+            g.wait_ge(T.sem["arr%d" % s], cnt[(core, s)])
+        slot = T.wall[:, s * WB:(s + 1) * WB]
+        lst = []
+        for ds, en in trs:
+            ids = []
+            for x in ds:
+                rid, pid = topo.addr(x, core)
+                ids.append(DstId(rid=rid, pnc=pid))
+            lst.append(RemoteDMATransfer(dst_ids=ids, dma_engine_mask=_mask(en), remote_sem=T.sem["arr%d" % s],
+                                         srcs=[slot], dsts=[slot for _ in ds], alu_op=0))
+            total += len(en)
+        g.remote_dma_fused(lst, local_sem=T.sem.snd)
+    g.wait_ge(T.sem.snd, total)
+
+
+def _compute(g, core, T, r, order, cnt):
+    sem, te, ve, sy, sc = T.sem, g.tensor, g.vector, g.sync, g.scalar
+    route = T.tables["ROUTE"][r]
+    KG = 65
+
+    def w(e, j):
+        return T.wall[:, e * WB + j * D:e * WB + (j + 1) * D]
+
+    sy.dma_start(w(r, 0), T.w1[:, :]).then_inc(sem.ldw, 16)
+    sc.dma_start(w(r, 1), T.w2[:, :]).then_inc(sem.ldw, 16)
+    sc.wait_ge(sem.gz, 1)
+    sc.dma_start(T.gsb[0:KG:32, :], T.gate[:, :]).then_inc(sem.ldg, 16)
+    sy.dma_start(T.xsb[:, :], T.x[:, :]).then_inc(sem.ldx, 16)
+    sc.wait_ge(sem.on, 1)
+    sc.dma_start(T.ed[:, 0, :], T.ones[0:NR, :]).then_inc(sem.edw, 16)
+    sy.wait_ge(sem.zr, 1)
+    sy.dma_start(T.ed[:, 1:NR + 1, :], T.zero[0:NR * NR * D // TOKN, :]).then_inc(sem.edw, 16)
+    sy.wait_ge(sem.edw, 32)
+    sy.dma_start(T.esb[0:NR + 1, :], T.ed[:, :, :]).then_inc(sem.esr, 16)
+
+    ve.memset(T.gsb[0:KG, :], 0.0).then_inc(sem.gz, 1)
+    ve.memset(T.ones[0:NR, :], 1.0).then_inc(sem.on, 1)
+    ve.memset(T.zero[:, :], 0.0).then_inc(sem.zr, 1)
+    ve.memset(T.tab[0:KG, :], 0.0).then_inc(sem.tz, 1)
+    ve.wait_ge(sem.tz, 1)
+    ntab = 1
+    ve.memset(T.tab[0:1, WIN - 1:WIN + WIN * (len(SECS) - 1):WIN], 1.0).then_inc(sem.tb, 1)
+    for d2 in range(2, NR):
+        a0 = WIN - 1 + WIN * SECS[(1, d2)]
+        n = d2 - 1
+        ve.memset(T.tab[32:33, a0 + 1:a0 + 2 + (WIN + 1) * (n - 1):WIN + 1], 1.0).then_inc(sem.tb, 1)
+        ve.memset(T.tab[64:65, a0 + d2:a0 + d2 + 1 + WIN * (n - 1):WIN], 1.0).then_inc(sem.tb, 1)
+        ntab += 2
+
+    zb, gb, hb, ya = [T.zb0, T.zb1], [T.gb0, T.gb1], [T.h0, T.h1], [T.ya0, T.ya1]
+
+    def cols(c):
+        return slice(c * CW, (c + 1) * CW)
+
+    def mm_z(u):
+        e, c = order[u // NH], u % NH
+        te.matmul(zb[u % 2][:, 0:CW], w(e, 0), T.xsb[:, cols(c)], start=True, stop=True).then_inc(sem["z%d" % u], 1)
+
+    def mm_y(u):
+        k, c = u // NH, u % NH
+        te.wait_ge(sem["hs%d" % u], 1)
+        te.matmul(ya[c][:, 0:CW], w(order[k], 1), T.hs[:, u * CW:(u + 1) * CW], start=(k == 0), stop=(k == NR - 1)).then_inc(sem["yc%d" % c], 1)
+
+    te.wait_ge(sem.ldw, 32)
+    te.wait_ge(sem.ldx, 16)
+    for u in range(NH):
+        mm_z(u)
+    te.wait_ge(sem.tb, ntab)
+    te.wait_ge(sem.ldg, 16)
+    classes = {}
+    for t, tr in enumerate(route):
+        classes.setdefault(tuple(tr), []).append(t)
+    ng = 0
+    for (e1, e2, e3), ts in sorted(classes.items()):
+        s0 = WIN - 1 + WIN * SECS[(e2 - e1, e3 - e1)] - e1
+        for i in range(0, len(ts), 2):
+            pr = ts[i:i + 2]
+            sl = slice(pr[0], pr[0] + 1) if len(pr) == 1 else slice(pr[0], pr[1] + 1, pr[1] - pr[0])
+            te.matmul(T.gps[0:NR, sl], T.tab[0:KG, s0:s0 + NR], T.gsb[0:KG, sl], start=True, stop=True).then_inc(sem.gg, 1)
+            ng += 1
+    te.wait_ge(sem.gcp, 1)
+    te.wait_ge(sem.esr, 16)
+    for u in range(NU):
+        e, c = order[u // NH], u % NH
+        if u >= 2:
+            te.wait_ge(sem["hs%d" % (u - 2)], 1)
+        te.matmul(gb[u % 2][:, 0:CW], T.esb[0:NR, e * D:(e + 1) * D], T.gs[0:NR, cols(c)], start=True, stop=True).then_inc(sem["gb%d" % u], 1)
+        if u >= NH:
+            if c == 0:
+                te.wait_ge(sem["arr%d" % e], cnt[(core, e)])
+            mm_z(u)
+        if u >= 1:
+            mm_y(u - 1)
+    mm_y(NU - 1)
+
+    def relu(u):
+        ve.wait_ge(sem["z%d" % u], 1)
+        if u >= 2:
+            ve.wait_ge(sem["hs%d" % (u - 2)], 1)
+        ve.tensor_tensor(hb[u % 2][:, :], zb[u % 2][:, 0:CW], T.zero[:, 0:CW], AluOpType.max).then_inc(sem["rl%d" % u], 1)
+
+    def mult(u):
+        ve.wait_ge(sem["rl%d" % u], 1)
+        ve.wait_ge(sem["gb%d" % u], 1)
+        ve.tensor_tensor(T.hs[:, u * CW:(u + 1) * CW], hb[u % 2][:, :], gb[u % 2][:, 0:CW], AluOpType.mult).then_inc(sem["hs%d" % u], 1)
+
+    ve.wait_ge(sem.zr, 1)
+    for u in range(NH):
+        relu(u)
+    ve.wait_ge(sem.gg, ng)
+    ve.tensor_copy(T.gs[0:NR, :], T.gps[0:NR, :]).then_inc(sem.gcp, 1)
+    for u in range(NH):
+        mult(u)
+    for u in range(NH, NU):
+        relu(u)
+        mult(u)
+    for c in range(NH):
+        ve.wait_ge(sem["yc%d" % c], NR)
+        ve.tensor_copy(T.ysb[:, cols(c)], ya[c][:, 0:CW]).then_inc(sem["cp%d" % c], 1)
+        q = sy if c % 2 == 0 else sc
+        q.wait_ge(sem["cp%d" % c], 1)
+        q.dma_start(T.y[:, cols(c)], T.ysb[:, cols(c)]).then_inc(sem["st%d" % c], 16)
+        q.wait_ge(sem["st%d" % c], 16)
+
+
+def rank_program(g, core, T, topo):
+    calls, cnt, order = _plan(T, topo)
+    rank = T.rank_of(core)
+    if rank is not None:
+        _compute(g, core, T, rank, order[rank], cnt)
+    if core in calls:
+        _send(g, core, T, topo, calls[core], cnt, rank)

@@ -8,6 +8,7 @@ WB = 2 * D
 NH = 2
 CW = TOKN // NH
 NU = NR * NH
+RB = 4
 WIN = 12
 SECS = {}
 for _d2 in range(2, NR):
@@ -20,19 +21,21 @@ SCRATCH = {
     "xsb": ("sbuf", [128, TOKN], "bfloat16"),
     "gsb": ("sbuf", [128, TOKN], "bfloat16"),
     "tab": ("sbuf", [128, TABL], "bfloat16"),
-    "zero": ("sbuf", [128, TOKN], "bfloat16"),
+    "zero": ("sbuf", [128, CW], "bfloat16"),
     "ones": ("sbuf", [128, D], "bfloat16"),
     "ed": ("dram", [NR, NR + 1, D], "bfloat16"),
     "esb": ("sbuf", [128, NR * D], "bfloat16"),
     "gs": ("sbuf", [128, TOKN], "bfloat16"),
     "h0": ("sbuf", [128, CW], "bfloat16"),
     "h1": ("sbuf", [128, CW], "bfloat16"),
+    "h2": ("sbuf", [128, CW], "bfloat16"),
+    "h3": ("sbuf", [128, CW], "bfloat16"),
     "hs": ("sbuf", [128, NU * CW], "bfloat16"),
     "ysb": ("sbuf", [128, TOKN], "bfloat16"),
-    "zb0": ("psum", [128, 512], "float32"),
-    "zb1": ("psum", [128, 512], "float32"),
-    "gb0": ("psum", [128, 512], "float32"),
-    "gb1": ("psum", [128, 512], "float32"),
+    "ub0": ("psum", [128, 512], "float32"),
+    "ub1": ("psum", [128, 512], "float32"),
+    "ub2": ("psum", [128, 512], "float32"),
+    "ub3": ("psum", [128, 512], "float32"),
     "ya0": ("psum", [128, 512], "float32"),
     "ya1": ("psum", [128, 512], "float32"),
     "gps": ("psum", [128, 512], "float32"),
@@ -149,6 +152,7 @@ def _compute(g, core, T, r, order, cnt):
     sem, te, ve, sy, sc = T.sem, g.tensor, g.vector, g.sync, g.scalar
     route = T.tables["ROUTE"][r]
     KG = 65
+    NZ = NR * NR * D // TOKN
 
     def w(e, j):
         return T.wall[:, e * WB + j * D:e * WB + (j + 1) * D]
@@ -158,16 +162,15 @@ def _compute(g, core, T, r, order, cnt):
     sc.wait_ge(sem.gz, 1)
     sc.dma_start(T.gsb[0:KG:32, :], T.gate[:, :]).then_inc(sem.ldg, 16)
     sy.dma_start(T.xsb[:, :], T.x[:, :]).then_inc(sem.ldx, 16)
+    sy.wait_ge(sem.gz, 1)
+    sy.dma_start(T.ed[:, 1:NR + 1, :], T.gsb[KG:KG + NZ, :]).then_inc(sem.edw, 16)
     sc.wait_ge(sem.on, 1)
     sc.dma_start(T.ed[:, 0, :], T.ones[0:NR, :]).then_inc(sem.edw, 16)
-    sy.wait_ge(sem.zr, 1)
-    sy.dma_start(T.ed[:, 1:NR + 1, :], T.zero[0:NR * NR * D // TOKN, :]).then_inc(sem.edw, 16)
     sy.wait_ge(sem.edw, 32)
     sy.dma_start(T.esb[0:NR + 1, :], T.ed[:, :, :]).then_inc(sem.esr, 16)
 
-    ve.memset(T.gsb[0:KG, :], 0.0).then_inc(sem.gz, 1)
+    ve.memset(T.gsb[:, :], 0.0).then_inc(sem.gz, 1)
     ve.memset(T.ones[0:NR, :], 1.0).then_inc(sem.on, 1)
-    ve.memset(T.zero[:, :], 0.0).then_inc(sem.zr, 1)
     ve.memset(T.tab[0:KG, :], 0.0).then_inc(sem.tz, 1)
     ve.wait_ge(sem.tz, 1)
     ntab = 1
@@ -178,15 +181,20 @@ def _compute(g, core, T, r, order, cnt):
         ve.memset(T.tab[32:33, a0 + 1:a0 + 2 + (WIN + 1) * (n - 1):WIN + 1], 1.0).then_inc(sem.tb, 1)
         ve.memset(T.tab[64:65, a0 + d2:a0 + d2 + 1 + WIN * (n - 1):WIN], 1.0).then_inc(sem.tb, 1)
         ntab += 2
+    ve.memset(T.zero[:, :], 0.0).then_inc(sem.zr, 1)
 
-    zb, gb, hb, ya = [T.zb0, T.zb1], [T.gb0, T.gb1], [T.h0, T.h1], [T.ya0, T.ya1]
+    ub, hb, ya = [T.ub0, T.ub1, T.ub2, T.ub3], [T.h0, T.h1, T.h2, T.h3], [T.ya0, T.ya1]
 
     def cols(c):
         return slice(c * CW, (c + 1) * CW)
 
     def mm_z(u):
         e, c = order[u // NH], u % NH
-        te.matmul(zb[u % 2][:, 0:CW], w(e, 0), T.xsb[:, cols(c)], start=True, stop=True).then_inc(sem["z%d" % u], 1)
+        te.matmul(ub[u % RB][:, 0:CW], w(e, 0), T.xsb[:, cols(c)], start=True, stop=True).then_inc(sem["z%d" % u], 1)
+
+    def mm_g(u):
+        e, c = order[u // NH], u % NH
+        te.matmul(ub[u % RB][:, CW:2 * CW], T.esb[0:NR, e * D:(e + 1) * D], T.gs[0:NR, cols(c)], start=True, stop=True).then_inc(sem["gb%d" % u], 1)
 
     def mm_y(u):
         k, c = u // NH, u % NH
@@ -212,29 +220,35 @@ def _compute(g, core, T, r, order, cnt):
             ng += 1
     te.wait_ge(sem.gcp, 1)
     te.wait_ge(sem.esr, 16)
-    for u in range(NU):
-        e, c = order[u // NH], u % NH
-        if u >= 2:
-            te.wait_ge(sem["hs%d" % (u - 2)], 1)
-        te.matmul(gb[u % 2][:, 0:CW], T.esb[0:NR, e * D:(e + 1) * D], T.gs[0:NR, cols(c)], start=True, stop=True).then_inc(sem["gb%d" % u], 1)
-        if u >= NH:
-            if c == 0:
-                te.wait_ge(sem["arr%d" % e], cnt[(core, e)])
-            mm_z(u)
-        if u >= 1:
-            mm_y(u - 1)
-    mm_y(NU - 1)
+    for k in range(NR):
+        us = [k * NH + c for c in range(NH)]
+        for u in us:
+            if u >= RB:
+                te.wait_ge(sem["hs%d" % (u - RB)], 1)
+            if k == 0:
+                te.wait_ge(sem["rl%d" % u], 1)
+            mm_g(u)
+        if k > 0:
+            te.wait_ge(sem["arr%d" % order[k]], cnt[(core, order[k])])
+            for u in us:
+                mm_z(u)
+            for u in us:
+                mm_y(u - NH)
+    for u in range(NU - NH, NU):
+        mm_y(u)
 
     def relu(u):
         ve.wait_ge(sem["z%d" % u], 1)
-        if u >= 2:
-            ve.wait_ge(sem["hs%d" % (u - 2)], 1)
-        ve.tensor_tensor(hb[u % 2][:, :], zb[u % 2][:, 0:CW], T.zero[:, 0:CW], AluOpType.max).then_inc(sem["rl%d" % u], 1)
+        if u >= NH:
+            ve.wait_ge(sem["gb%d" % u], 1)
+        if u >= RB:
+            ve.wait_ge(sem["hs%d" % (u - RB)], 1)
+        ve.tensor_tensor(hb[u % RB][:, :], ub[u % RB][:, 0:CW], T.zero[:, :], AluOpType.max).then_inc(sem["rl%d" % u], 1)
 
     def mult(u):
         ve.wait_ge(sem["rl%d" % u], 1)
         ve.wait_ge(sem["gb%d" % u], 1)
-        ve.tensor_tensor(T.hs[:, u * CW:(u + 1) * CW], hb[u % 2][:, :], gb[u % 2][:, 0:CW], AluOpType.mult).then_inc(sem["hs%d" % u], 1)
+        ve.tensor_tensor(T.hs[:, u * CW:(u + 1) * CW], hb[u % RB][:, :], ub[u % RB][:, CW:2 * CW], AluOpType.mult).then_inc(sem["hs%d" % u], 1)
 
     ve.wait_ge(sem.zr, 1)
     for u in range(NH):
@@ -243,9 +257,11 @@ def _compute(g, core, T, r, order, cnt):
     ve.tensor_copy(T.gs[0:NR, :], T.gps[0:NR, :]).then_inc(sem.gcp, 1)
     for u in range(NH):
         mult(u)
-    for u in range(NH, NU):
-        relu(u)
-        mult(u)
+    for k in range(1, NR):
+        for c in range(NH):
+            relu(k * NH + c)
+        for c in range(NH):
+            mult(k * NH + c)
     for c in range(NH):
         ve.wait_ge(sem["yc%d" % c], NR)
         ve.tensor_copy(T.ysb[:, cols(c)], ya[c][:, 0:CW]).then_inc(sem["cp%d" % c], 1)

@@ -4,10 +4,14 @@ from concourse.mybir import AluOpType
 NR = 12
 D = 128
 TOKN = 512
+KS = 3
+GC = 16
+GP = KS * TOKN // GC
+XW = TOKN + GC
 WB = 2 * D
 NH = 2
 CW = TOKN // NH
-NU = NR * NH
+NU = NR * NH // 2
 RB = 4
 WIN = 12
 SECS = {}
@@ -18,7 +22,7 @@ TABL = 688
 
 SCRATCH = {
     "wall": ("sbuf", [128, NR * WB], "bfloat16"),
-    "xsb": ("sbuf", [128, TOKN], "bfloat16"),
+    "xg": ("sbuf", [128, XW], "bfloat16"),
     "gsb": ("sbuf", [128, TOKN], "bfloat16"),
     "tab": ("sbuf", [128, TABL], "bfloat16"),
     "zero": ("sbuf", [128, CW], "bfloat16"),
@@ -32,6 +36,7 @@ SCRATCH = {
     "h3": ("sbuf", [128, CW], "bfloat16"),
     "hs": ("sbuf", [128, NU * CW], "bfloat16"),
     "ysb": ("sbuf", [128, TOKN], "bfloat16"),
+    "part": ("sbuf", [128, 2 * TOKN], "bfloat16"),
     "ub0": ("psum", [128, 512], "float32"),
     "ub1": ("psum", [128, 512], "float32"),
     "ub2": ("psum", [128, 512], "float32"),
@@ -42,8 +47,8 @@ SCRATCH = {
 }
 SEMAPHORES = (["arr%d" % s for s in range(NR)]
               + ["%s%d" % (n, u) for n in ("z", "gb", "rl", "hs") for u in range(NU)]
-              + ["%s%d" % (n, c) for n in ("yc", "cp", "st") for c in range(NH)]
-              + ["ldw", "ldx", "ldg", "gz", "on", "zr", "tz", "tb", "gg", "gcp", "edw", "esr", "snd"])
+              + ["%s%d" % (n, c) for n in ("yc", "cp", "st", "ad", "pa0", "pa1") for c in range(NH)]
+              + ["ldw", "ldx", "ldp", "ldg", "gz", "on", "zr", "tz", "tb", "gg", "gcp", "gpz", "edw", "esr", "snd", "xa"])
 
 _CACHE = {}
 
@@ -84,27 +89,38 @@ def _plan(T, topo):
     for S in cores:
         twin.append([t for t, X in enumerate(cores) if topo.rack(topo.host(X)) != topo.rack(topo.host(S))
                      and topo.chip(X) == topo.chip(S) and topo.may_write(S, X)][0])
-    calls, cnt, klass = {}, {}, {}
+    calls, cnt, key = {}, {}, {}
+    mine = {}
     second = []
     for s, S in enumerate(cores):
         tw = twin[s]
+        place = [x for x in cores if topo.host(x) == topo.host(S)].index(S)
         direct, viaP, viaQ, farP, farQ = [], [], [], [], []
         for d, X in enumerate(cores):
-            if d == s:
-                klass[(d, s)] = 0
-            elif topo.rack(topo.host(X)) == topo.rack(topo.host(S)):
-                if topo.may_write(S, X):
+            if topo.rack(topo.host(X)) == topo.rack(topo.host(S)):
+                mine.setdefault(X, []).append(s)
+                if d == s:
+                    key[(X, s)] = 0
+                elif topo.may_write(S, X):
                     direct.append(X)
-                    klass[(d, s)] = 1
+                    key[(X, s)] = 1
                 else:
                     (viaP if topo.host(X) == topo.host(S) else viaQ).append(X)
-                    klass[(d, s)] = 2
+                    key[(X, s)] = 2
             elif topo.host(X) == topo.host(cores[tw]):
-                farQ.append(X)
-                klass[(d, s)] = 3
+                mine.setdefault(Q[d], []).append(s)
+                farQ.append(Q[d])
             else:
-                farP.append(X)
-                klass[(d, s)] = 4
+                mine.setdefault(P[d], []).append(s)
+                farP.append(P[d])
+        i = farQ.index(Q[tw])
+        farQ = farQ[i + 1:] + farQ[:i]
+        key[(Q[tw], s)] = 0
+        i = place % len(farP)
+        farP = farP[i:] + farP[:i]
+        for lst in (farQ, farP):
+            for j, x in enumerate(lst):
+                key[(x, s)] = 1 + j
         off = _bits(topo.mask(S, P[tw]))
         onl = [e for e in _bits(topo.mask(S, P[s])) if e not in off]
         first = [([P[tw], Q[tw]], off[0::2]), (direct, off[1::2]),
@@ -122,64 +138,77 @@ def _plan(T, topo):
             for ds, en in trs:
                 for x in ds:
                     cnt[(x, s)] = len(en)
-    order = [sorted(range(len(cores)), key=lambda s: (klass[(d, s)], s)) for d in range(len(cores))]
-    _CACHE["p"] = (calls, cnt, order)
+    work, xsend, back = {}, {}, {}
+    for d, X in enumerate(cores):
+        off = _bits(topo.mask(X, P[twin[d]]))
+        xsend[X] = ([Q[d], P[d]], [e for e in _bits(topo.mask(X, P[d])) if e not in off])
+        for k, h in ((X, None), (Q[d], 0), (P[d], 1)):
+            lst = sorted(mine[k], key=lambda s: (key[(k, s)], s))
+            work[k] = (d, lst, h, key[(k, lst[0])] == 0)
+            if h is not None:
+                back[k] = (X, [e for e in _bits(topo.mask(k, X)) if e in off])
+    _CACHE["p"] = (calls, cnt, work, xsend, back)
     return _CACHE["p"]
 
 
-def _send(g, core, T, topo, calls, cnt, own):
-    total = 0
-    for s, trs in calls:
-        if s == own:
-            g.wait_ge(T.sem.ldw, 32)
-        else:
-            g.wait_ge(T.sem["arr%d" % s], cnt[(core, s)])
-        slot = T.wall[:, s * WB:(s + 1) * WB]
-        lst = []
-        for ds, en in trs:
-            ids = []
-            for x in ds:
-                rid, pid = topo.addr(x, core)
-                ids.append(DstId(rid=rid, pnc=pid))
-            lst.append(RemoteDMATransfer(dst_ids=ids, dma_engine_mask=_mask(en), remote_sem=T.sem["arr%d" % s],
-                                         srcs=[slot], dsts=[slot for _ in ds], alu_op=0))
-            total += len(en)
-        g.remote_dma_fused(lst, local_sem=T.sem.snd)
-    g.wait_ge(T.sem.snd, total)
+def _write(g, core, T, topo, trs, src, dst, rsem):
+    lst, total = [], 0
+    for ds, en in trs:
+        ids = []
+        for x in ds:
+            rid, pid = topo.addr(x, core)
+            ids.append(DstId(rid=rid, pnc=pid))
+        lst.append(RemoteDMATransfer(dst_ids=ids, dma_engine_mask=_mask(en), remote_sem=rsem,
+                                     srcs=[src], dsts=[dst for _ in ds], alu_op=0))
+        total += len(en)
+    g.remote_dma_fused(lst, local_sem=T.sem.snd)
+    return total
 
 
-def _compute(g, core, T, r, order, cnt):
+def _compute(g, core, T, r, mine, helper, early, cnt, nxa, nback):
     sem, te, ve, sy, sc = T.sem, g.tensor, g.vector, g.sync, g.scalar
     route = T.tables["ROUTE"][r]
     KG = 65
     NZ = NR * NR * D // TOKN
+    m = len(mine)
+    a0 = min(mine)
+    MW = max(mine) - a0 + 1
+    nu = m * NH
 
     def w(e, j):
         return T.wall[:, e * WB + j * D:e * WB + (j + 1) * D]
 
-    sy.dma_start(w(r, 0), T.w1[:, :]).then_inc(sem.ldw, 16)
-    sc.dma_start(w(r, 1), T.w2[:, :]).then_inc(sem.ldw, 16)
-    sc.wait_ge(sem.gz, 1)
-    sc.dma_start(T.gsb[0:KG:32, :], T.gate[:, :]).then_inc(sem.ldg, 16)
-    sy.dma_start(T.xsb[:, :], T.x[:, :]).then_inc(sem.ldx, 16)
+    if helper is None:
+        sy.dma_start(w(r, 0), T.w1[:, :]).then_inc(sem.ldw, 16)
+        sc.dma_start(w(r, 1), T.w2[:, :]).then_inc(sem.ldw, 16)
+        sy.dma_start(T.xg[:, 0:TOKN], T.x[:, :]).then_inc(sem.ldx, 16)
+        sc.dma_start(T.xg[0:GP, TOKN:XW], T.gate[:, :]).then_inc(sem.ldp, 16)
+        sc.dma_start(T.xg[GP:128, TOKN:XW], T.gate[0:1, :]).then_inc(sem.ldp, 16)
+        sc.wait_ge(sem.gz, 1)
+        sc.dma_start(T.gsb[0:KG:32, :], T.gate[:, :]).then_inc(sem.ldg, 16)
     sy.wait_ge(sem.gz, 1)
     sy.dma_start(T.ed[:, 1:NR + 1, :], T.gsb[KG:KG + NZ, :]).then_inc(sem.edw, 16)
     sc.wait_ge(sem.on, 1)
     sc.dma_start(T.ed[:, 0, :], T.ones[0:NR, :]).then_inc(sem.edw, 16)
+    if helper is not None:
+        sc.wait_ge(sem.gz, 1)
+        sc.wait_ge(sem.xa, nxa)
+        sc.dma_start(T.gsb[0:KG:32, :], T.xg[0:GP, TOKN:XW]).then_inc(sem.ldg, 16)
     sy.wait_ge(sem.edw, 32)
     sy.dma_start(T.esb[0:NR + 1, :], T.ed[:, :, :]).then_inc(sem.esr, 16)
 
     ve.memset(T.gsb[:, :], 0.0).then_inc(sem.gz, 1)
     ve.memset(T.ones[0:NR, :], 1.0).then_inc(sem.on, 1)
     ve.memset(T.tab[0:KG, :], 0.0).then_inc(sem.tz, 1)
+    ve.memset(T.gps[0:MW, :], 0.0).then_inc(sem.gpz, 1)
     ve.wait_ge(sem.tz, 1)
     ntab = 1
     ve.memset(T.tab[0:1, WIN - 1:WIN + WIN * (len(SECS) - 1):WIN], 1.0).then_inc(sem.tb, 1)
     for d2 in range(2, NR):
-        a0 = WIN - 1 + WIN * SECS[(1, d2)]
+        b0 = WIN - 1 + WIN * SECS[(1, d2)]
         n = d2 - 1
-        ve.memset(T.tab[32:33, a0 + 1:a0 + 2 + (WIN + 1) * (n - 1):WIN + 1], 1.0).then_inc(sem.tb, 1)
-        ve.memset(T.tab[64:65, a0 + d2:a0 + d2 + 1 + WIN * (n - 1):WIN], 1.0).then_inc(sem.tb, 1)
+        ve.memset(T.tab[32:33, b0 + 1:b0 + 2 + (WIN + 1) * (n - 1):WIN + 1], 1.0).then_inc(sem.tb, 1)
+        ve.memset(T.tab[64:65, b0 + d2:b0 + d2 + 1 + WIN * (n - 1):WIN], 1.0).then_inc(sem.tb, 1)
         ntab += 2
     ve.memset(T.zero[:, :], 0.0).then_inc(sem.zr, 1)
 
@@ -188,58 +217,74 @@ def _compute(g, core, T, r, order, cnt):
     def cols(c):
         return slice(c * CW, (c + 1) * CW)
 
+    def block(k):
+        e = mine[k]
+        if helper is None and e == r:
+            te.wait_ge(sem.ldw, 32)
+        else:
+            te.wait_ge(sem["arr%d" % e], cnt[(core, e)])
+
     def mm_z(u):
-        e, c = order[u // NH], u % NH
-        te.matmul(ub[u % RB][:, 0:CW], w(e, 0), T.xsb[:, cols(c)], start=True, stop=True).then_inc(sem["z%d" % u], 1)
+        e, c = mine[u // NH], u % NH
+        te.matmul(ub[u % RB][:, 0:CW], w(e, 0), T.xg[:, cols(c)], start=True, stop=True).then_inc(sem["z%d" % u], 1)
 
     def mm_g(u):
-        e, c = order[u // NH], u % NH
-        te.matmul(ub[u % RB][:, CW:2 * CW], T.esb[0:NR, e * D:(e + 1) * D], T.gs[0:NR, cols(c)], start=True, stop=True).then_inc(sem["gb%d" % u], 1)
+        e, c = mine[u // NH], u % NH
+        te.matmul(ub[u % RB][:, CW:2 * CW], T.esb[0:MW, (e - a0) * D:(e - a0 + 1) * D], T.gs[0:MW, cols(c)], start=True, stop=True).then_inc(sem["gb%d" % u], 1)
 
     def mm_y(u):
         k, c = u // NH, u % NH
         te.wait_ge(sem["hs%d" % u], 1)
-        te.matmul(ya[c][:, 0:CW], w(order[k], 1), T.hs[:, u * CW:(u + 1) * CW], start=(k == 0), stop=(k == NR - 1)).then_inc(sem["yc%d" % c], 1)
+        te.matmul(ya[c][:, 0:CW], w(mine[k], 1), T.hs[:, u * CW:(u + 1) * CW], start=(k == 0), stop=(k == m - 1)).then_inc(sem["yc%d" % c], 1)
 
-    te.wait_ge(sem.ldw, 32)
-    te.wait_ge(sem.ldx, 16)
-    for u in range(NH):
-        mm_z(u)
+    if helper is None:
+        te.wait_ge(sem.ldx, 16)
+    else:
+        te.wait_ge(sem.xa, nxa)
+    if early:
+        block(0)
+        for u in range(NH):
+            mm_z(u)
     te.wait_ge(sem.tb, ntab)
+    te.wait_ge(sem.gpz, 1)
     te.wait_ge(sem.ldg, 16)
     classes = {}
     for t, tr in enumerate(route):
-        classes.setdefault(tuple(tr), []).append(t)
+        kk = tuple((i, e) for i, e in enumerate(tr) if a0 <= e < a0 + MW)
+        if kk:
+            classes.setdefault(kk, []).append(t)
     ng = 0
-    for (e1, e2, e3), ts in sorted(classes.items()):
-        s0 = WIN - 1 + WIN * SECS[(e2 - e1, e3 - e1)] - e1
+    for kk, ts in sorted(classes.items()):
+        e1, e2, e3 = route[ts[0]]
+        s0 = WIN - 1 + WIN * SECS[(e2 - e1, e3 - e1)] - e1 + a0
         for i in range(0, len(ts), 2):
             pr = ts[i:i + 2]
             sl = slice(pr[0], pr[0] + 1) if len(pr) == 1 else slice(pr[0], pr[1] + 1, pr[1] - pr[0])
-            te.matmul(T.gps[0:NR, sl], T.tab[0:KG, s0:s0 + NR], T.gsb[0:KG, sl], start=True, stop=True).then_inc(sem.gg, 1)
+            te.matmul(T.gps[0:MW, sl], T.tab[0:KG, s0:s0 + MW], T.gsb[0:KG, sl], start=True, stop=True).then_inc(sem.gg, 1)
             ng += 1
     te.wait_ge(sem.gcp, 1)
     te.wait_ge(sem.esr, 16)
-    for k in range(NR):
+    for k in range(m):
         us = [k * NH + c for c in range(NH)]
         for u in us:
             if u >= RB:
                 te.wait_ge(sem["hs%d" % (u - RB)], 1)
-            if k == 0:
+            if k == 0 and early:
                 te.wait_ge(sem["rl%d" % u], 1)
             mm_g(u)
-        if k > 0:
-            te.wait_ge(sem["arr%d" % order[k]], cnt[(core, order[k])])
+        if k > 0 or not early:
+            block(k)
             for u in us:
                 mm_z(u)
+        if k > 0:
             for u in us:
                 mm_y(u - NH)
-    for u in range(NU - NH, NU):
+    for u in range(nu - NH, nu):
         mm_y(u)
 
     def relu(u):
         ve.wait_ge(sem["z%d" % u], 1)
-        if u >= NH:
+        if u >= NH or not early:
             ve.wait_ge(sem["gb%d" % u], 1)
         if u >= RB:
             ve.wait_ge(sem["hs%d" % (u - RB)], 1)
@@ -251,20 +296,29 @@ def _compute(g, core, T, r, order, cnt):
         ve.tensor_tensor(T.hs[:, u * CW:(u + 1) * CW], hb[u % RB][:, :], ub[u % RB][:, CW:2 * CW], AluOpType.mult).then_inc(sem["hs%d" % u], 1)
 
     ve.wait_ge(sem.zr, 1)
-    for u in range(NH):
-        relu(u)
+    if early:
+        for u in range(NH):
+            relu(u)
     ve.wait_ge(sem.gg, ng)
-    ve.tensor_copy(T.gs[0:NR, :], T.gps[0:NR, :]).then_inc(sem.gcp, 1)
-    for u in range(NH):
-        mult(u)
-    for k in range(1, NR):
+    ve.tensor_copy(T.gs[0:MW, :], T.gps[0:MW, :]).then_inc(sem.gcp, 1)
+    if early:
+        for u in range(NH):
+            mult(u)
+    for k in range(1 if early else 0, m):
         for c in range(NH):
             relu(k * NH + c)
         for c in range(NH):
             mult(k * NH + c)
     for c in range(NH):
-        ve.wait_ge(sem["yc%d" % c], NR)
-        ve.tensor_copy(T.ysb[:, cols(c)], ya[c][:, 0:CW]).then_inc(sem["cp%d" % c], 1)
+        ve.wait_ge(sem["yc%d" % c], m)
+        if helper is not None:
+            ve.tensor_copy(T.ysb[:, cols(c)], ya[c][:, 0:CW]).then_inc(sem["cp%d" % c], 1)
+            continue
+        ve.wait_ge(sem["pa0%d" % c], nback)
+        ve.tensor_tensor(ya[c][:, 0:CW], ya[c][:, 0:CW], T.part[:, c * CW:(c + 1) * CW], AluOpType.add).then_inc(sem["ad%d" % c], 1)
+        ve.wait_ge(sem["ad%d" % c], 1)
+        ve.wait_ge(sem["pa1%d" % c], nback)
+        ve.tensor_tensor(T.ysb[:, cols(c)], ya[c][:, 0:CW], T.part[:, (NH + c) * CW:(NH + c + 1) * CW], AluOpType.add).then_inc(sem["cp%d" % c], 1)
         q = sy if c % 2 == 0 else sc
         q.wait_ge(sem["cp%d" % c], 1)
         q.dma_start(T.y[:, cols(c)], T.ysb[:, cols(c)]).then_inc(sem["st%d" % c], 16)
@@ -272,9 +326,30 @@ def _compute(g, core, T, r, order, cnt):
 
 
 def rank_program(g, core, T, topo):
-    calls, cnt, order = _plan(T, topo)
-    rank = T.rank_of(core)
-    if rank is not None:
-        _compute(g, core, T, rank, order[rank], cnt)
-    if core in calls:
-        _send(g, core, T, topo, calls[core], cnt, rank)
+    calls, cnt, work, xsend, back = _plan(T, topo)
+    if core not in work:
+        return
+    r, mine, helper, early = work[core]
+    rankcore = T.cores[r]
+    nxa = len(xsend[rankcore][1])
+    nback = len(back[xsend[rankcore][0][0]][1])
+    _compute(g, core, T, r, mine, helper, early, cnt, nxa, nback)
+    total = 0
+    for s, trs in calls.get(core, []):
+        if helper is None:
+            g.wait_ge(T.sem.ldw, 32)
+        else:
+            g.wait_ge(T.sem["arr%d" % s], cnt[(core, s)])
+        slot = T.wall[:, s * WB:(s + 1) * WB]
+        total += _write(g, core, T, topo, trs, slot, slot, T.sem["arr%d" % s])
+    if helper is None:
+        g.wait_ge(T.sem.ldx, 16)
+        g.wait_ge(T.sem.ldp, 32)
+        total += _write(g, core, T, topo, [xsend[core]], T.xg[:, 0:XW], T.xg[:, 0:XW], T.sem.xa)
+    else:
+        home, en = back[core]
+        for c in range(NH):
+            g.wait_ge(T.sem["cp%d" % c], 1)
+            total += _write(g, core, T, topo, [([home], en)], T.ysb[:, c * CW:(c + 1) * CW],
+                            T.part[:, (helper * NH + c) * CW:(helper * NH + c + 1) * CW], T.sem["pa%d%d" % (helper, c)])
+    g.wait_ge(T.sem.snd, total)

from concourse.bass import DstId, RemoteDMATransfer
from concourse.mybir import AluOpType

NR = 12
D = 128
TOKN = 512
KS = 3
GC = 16
GP = KS * TOKN // GC
XW = TOKN + GC
WB = 2 * D
NH = 2
CW = TOKN // NH
NU = NR * NH // 2
RB = 4
WIN = 12
SECS = {}
for _d2 in range(2, NR):
    for _d1 in range(1, _d2):
        SECS[(_d1, _d2)] = len(SECS)
TABL = 688

SCRATCH = {
    "wall": ("sbuf", [128, NR * WB], "bfloat16"),
    "xg": ("sbuf", [128, XW], "bfloat16"),
    "gsb": ("sbuf", [128, TOKN], "bfloat16"),
    "tab": ("sbuf", [128, TABL], "bfloat16"),
    "zero": ("sbuf", [128, CW], "bfloat16"),
    "ones": ("sbuf", [128, D], "bfloat16"),
    "ed": ("dram", [NR, NR + 1, D], "bfloat16"),
    "esb": ("sbuf", [128, NR * D], "bfloat16"),
    "gs": ("sbuf", [128, TOKN], "bfloat16"),
    "h0": ("sbuf", [128, CW], "bfloat16"),
    "h1": ("sbuf", [128, CW], "bfloat16"),
    "h2": ("sbuf", [128, CW], "bfloat16"),
    "h3": ("sbuf", [128, CW], "bfloat16"),
    "hs": ("sbuf", [128, NU * CW], "bfloat16"),
    "ysb": ("sbuf", [128, TOKN], "bfloat16"),
    "part": ("sbuf", [128, 2 * TOKN], "bfloat16"),
    "ub0": ("psum", [128, 512], "float32"),
    "ub1": ("psum", [128, 512], "float32"),
    "ub2": ("psum", [128, 512], "float32"),
    "ub3": ("psum", [128, 512], "float32"),
    "ya0": ("psum", [128, 512], "float32"),
    "ya1": ("psum", [128, 512], "float32"),
    "gps": ("psum", [128, 512], "float32"),
}
SEMAPHORES = (["arr%d" % s for s in range(NR)]
              + ["%s%d" % (n, u) for n in ("z", "gb", "rl", "hs") for u in range(NU)]
              + ["%s%d" % (n, c) for n in ("yc", "cp", "st", "ad", "pa0", "pa1") for c in range(NH)]
              + ["ldw", "ldx", "ldp", "ldg", "gz", "on", "zr", "tz", "tb", "gg", "gcp", "gpz", "edw", "esr", "snd", "xa"])

_CACHE = {}


def _bits(m):
    return [i for i in range(m.bit_length()) if (m >> i) & 1]


def _mask(engs):
    m = 0
    for e in engs:
        m |= 1 << e
    return m


def _plan(T, topo):
    if "p" in _CACHE:
        return _CACHE["p"]
    cores = list(T.cores)
    nworld = topo.CORES_PER_HOST * (max(topo.host(c) for c in cores) + 1)

    def linked(a, b):
        return any(topo.may_write(u, v) for u in cores if topo.host(u) == a for v in cores if topo.host(v) == b and u != v)

    def relay(S, same_die):
        for k in range(nworld):
            if k in cores or topo.host(k) != topo.host(S) or topo.chip(k) != topo.chip(S):
                continue
            if (topo.die(k) == topo.die(S)) != same_die:
                continue
            if all(topo.may_write(k, d) for d in cores if linked(topo.host(k), topo.host(d))):
                return k
        return None

    P = [relay(S, False) for S in cores]
    Q = [relay(S, True) for S in cores]
    twin = []
    for S in cores:
        twin.append([t for t, X in enumerate(cores) if topo.rack(topo.host(X)) != topo.rack(topo.host(S))
                     and topo.chip(X) == topo.chip(S) and topo.may_write(S, X)][0])
    calls, cnt, key = {}, {}, {}
    mine = {}
    second = []
    for s, S in enumerate(cores):
        tw = twin[s]
        place = [x for x in cores if topo.host(x) == topo.host(S)].index(S)
        direct, viaP, viaQ, farP, farQ = [], [], [], [], []
        for d, X in enumerate(cores):
            if topo.rack(topo.host(X)) == topo.rack(topo.host(S)):
                mine.setdefault(X, []).append(s)
                if d == s:
                    key[(X, s)] = 0
                elif topo.may_write(S, X):
                    direct.append(X)
                    key[(X, s)] = 1
                else:
                    (viaP if topo.host(X) == topo.host(S) else viaQ).append(X)
                    key[(X, s)] = 2
            elif topo.host(X) == topo.host(cores[tw]):
                mine.setdefault(Q[d], []).append(s)
                farQ.append(Q[d])
            else:
                mine.setdefault(P[d], []).append(s)
                farP.append(P[d])
        i = farQ.index(Q[tw])
        farQ = farQ[i + 1:] + farQ[:i]
        key[(Q[tw], s)] = 0
        i = place % len(farP)
        farP = farP[i:] + farP[:i]
        for lst in (farQ, farP):
            for j, x in enumerate(lst):
                key[(x, s)] = 1 + j
        off = _bits(topo.mask(S, P[tw]))
        onl = [e for e in _bits(topo.mask(S, P[s])) if e not in off]
        first = [([P[tw], Q[tw]], off[0::2]), (direct, off[1::2]),
                 ([k for k, lst in ((P[s], viaP), (Q[s], viaQ)) if lst], onl)]
        calls[S] = [(s, [(ds, en) for ds, en in first if ds])]
        for k, lst in ((P[s], viaP), (Q[s], viaQ)):
            if lst:
                calls.setdefault(k, []).append((s, [(lst, _bits(topo.mask(k, lst[0])))]))
        for k, lst in ((P[tw], farP), (Q[tw], farQ)):
            second.append((k, (s, [(lst, [e for e in _bits(topo.mask(k, lst[0])) if all((topo.mask(k, x) >> e) & 1 for x in lst)])])))
    for k, c in second:
        calls.setdefault(k, []).append(c)
    for k, lst in calls.items():
        for s, trs in lst:
            for ds, en in trs:
                for x in ds:
                    cnt[(x, s)] = len(en)
    work, xsend, back = {}, {}, {}
    for d, X in enumerate(cores):
        off = _bits(topo.mask(X, P[twin[d]]))
        xsend[X] = ([Q[d], P[d]], [e for e in _bits(topo.mask(X, P[d])) if e not in off])
        for k, h in ((X, None), (Q[d], 0), (P[d], 1)):
            lst = sorted(mine[k], key=lambda s: (key[(k, s)], s))
            work[k] = (d, lst, h, key[(k, lst[0])] == 0)
            if h is not None:
                back[k] = (X, [e for e in _bits(topo.mask(k, X)) if e in off])
    _CACHE["p"] = (calls, cnt, work, xsend, back)
    return _CACHE["p"]


def _write(g, core, T, topo, trs, src, dst, rsem):
    lst, total = [], 0
    for ds, en in trs:
        ids = []
        for x in ds:
            rid, pid = topo.addr(x, core)
            ids.append(DstId(rid=rid, pnc=pid))
        lst.append(RemoteDMATransfer(dst_ids=ids, dma_engine_mask=_mask(en), remote_sem=rsem,
                                     srcs=[src], dsts=[dst for _ in ds], alu_op=0))
        total += len(en)
    g.remote_dma_fused(lst, local_sem=T.sem.snd)
    return total


def _compute(g, core, T, r, mine, helper, early, cnt, nxa, nback):
    sem, te, ve, sy, sc = T.sem, g.tensor, g.vector, g.sync, g.scalar
    route = T.tables["ROUTE"][r]
    KG = 65
    NZ = NR * NR * D // TOKN
    m = len(mine)
    a0 = min(mine)
    MW = max(mine) - a0 + 1
    nu = m * NH

    def w(e, j):
        return T.wall[:, e * WB + j * D:e * WB + (j + 1) * D]

    if helper is None:
        sy.dma_start(w(r, 0), T.w1[:, :]).then_inc(sem.ldw, 16)
        sc.dma_start(w(r, 1), T.w2[:, :]).then_inc(sem.ldw, 16)
        sy.dma_start(T.xg[:, 0:TOKN], T.x[:, :]).then_inc(sem.ldx, 16)
        sc.dma_start(T.xg[0:GP, TOKN:XW], T.gate[:, :]).then_inc(sem.ldp, 16)
        sc.dma_start(T.xg[GP:128, TOKN:XW], T.gate[0:1, :]).then_inc(sem.ldp, 16)
        sc.wait_ge(sem.gz, 1)
        sc.dma_start(T.gsb[0:KG:32, :], T.gate[:, :]).then_inc(sem.ldg, 16)
    sy.wait_ge(sem.gz, 1)
    sy.dma_start(T.ed[:, 1:NR + 1, :], T.gsb[KG:KG + NZ, :]).then_inc(sem.edw, 16)
    sc.wait_ge(sem.on, 1)
    sc.dma_start(T.ed[:, 0, :], T.ones[0:NR, :]).then_inc(sem.edw, 16)
    if helper is not None:
        sc.wait_ge(sem.gz, 1)
        sc.wait_ge(sem.xa, nxa)
        sc.dma_start(T.gsb[0:KG:32, :], T.xg[0:GP, TOKN:XW]).then_inc(sem.ldg, 16)
    sy.wait_ge(sem.edw, 32)
    sy.dma_start(T.esb[0:NR + 1, :], T.ed[:, :, :]).then_inc(sem.esr, 16)

    ve.memset(T.gsb[:, :], 0.0).then_inc(sem.gz, 1)
    ve.memset(T.ones[0:NR, :], 1.0).then_inc(sem.on, 1)
    ve.memset(T.tab[0:KG, :], 0.0).then_inc(sem.tz, 1)
    ve.memset(T.gps[0:MW, :], 0.0).then_inc(sem.gpz, 1)
    ve.wait_ge(sem.tz, 1)
    ntab = 1
    ve.memset(T.tab[0:1, WIN - 1:WIN + WIN * (len(SECS) - 1):WIN], 1.0).then_inc(sem.tb, 1)
    for d2 in range(2, NR):
        b0 = WIN - 1 + WIN * SECS[(1, d2)]
        n = d2 - 1
        ve.memset(T.tab[32:33, b0 + 1:b0 + 2 + (WIN + 1) * (n - 1):WIN + 1], 1.0).then_inc(sem.tb, 1)
        ve.memset(T.tab[64:65, b0 + d2:b0 + d2 + 1 + WIN * (n - 1):WIN], 1.0).then_inc(sem.tb, 1)
        ntab += 2
    ve.memset(T.zero[:, :], 0.0).then_inc(sem.zr, 1)

    ub, hb, ya = [T.ub0, T.ub1, T.ub2, T.ub3], [T.h0, T.h1, T.h2, T.h3], [T.ya0, T.ya1]

    def cols(c):
        return slice(c * CW, (c + 1) * CW)

    def block(k):
        e = mine[k]
        if helper is None and e == r:
            te.wait_ge(sem.ldw, 32)
        else:
            te.wait_ge(sem["arr%d" % e], cnt[(core, e)])

    def mm_z(u):
        e, c = mine[u // NH], u % NH
        te.matmul(ub[u % RB][:, 0:CW], w(e, 0), T.xg[:, cols(c)], start=True, stop=True).then_inc(sem["z%d" % u], 1)

    def mm_g(u):
        e, c = mine[u // NH], u % NH
        te.matmul(ub[u % RB][:, CW:2 * CW], T.esb[0:MW, (e - a0) * D:(e - a0 + 1) * D], T.gs[0:MW, cols(c)], start=True, stop=True).then_inc(sem["gb%d" % u], 1)

    def mm_y(u):
        k, c = u // NH, u % NH
        te.wait_ge(sem["hs%d" % u], 1)
        te.matmul(ya[c][:, 0:CW], w(mine[k], 1), T.hs[:, u * CW:(u + 1) * CW], start=(k == 0), stop=(k == m - 1)).then_inc(sem["yc%d" % c], 1)

    if helper is None:
        te.wait_ge(sem.ldx, 16)
    else:
        te.wait_ge(sem.xa, nxa)
    if early:
        block(0)
        for u in range(NH):
            mm_z(u)
    te.wait_ge(sem.tb, ntab)
    te.wait_ge(sem.gpz, 1)
    te.wait_ge(sem.ldg, 16)
    classes = {}
    for t, tr in enumerate(route):
        kk = tuple((i, e) for i, e in enumerate(tr) if a0 <= e < a0 + MW)
        if kk:
            classes.setdefault(kk, []).append(t)
    ng = 0
    for kk, ts in sorted(classes.items()):
        e1, e2, e3 = route[ts[0]]
        s0 = WIN - 1 + WIN * SECS[(e2 - e1, e3 - e1)] - e1 + a0
        for i in range(0, len(ts), 2):
            pr = ts[i:i + 2]
            sl = slice(pr[0], pr[0] + 1) if len(pr) == 1 else slice(pr[0], pr[1] + 1, pr[1] - pr[0])
            te.matmul(T.gps[0:MW, sl], T.tab[0:KG, s0:s0 + MW], T.gsb[0:KG, sl], start=True, stop=True).then_inc(sem.gg, 1)
            ng += 1
    te.wait_ge(sem.gcp, 1)
    te.wait_ge(sem.esr, 16)
    for k in range(m):
        us = [k * NH + c for c in range(NH)]
        for u in us:
            if u >= RB:
                te.wait_ge(sem["hs%d" % (u - RB)], 1)
            if k == 0 and early:
                te.wait_ge(sem["rl%d" % u], 1)
            mm_g(u)
        if k > 0 or not early:
            block(k)
            for u in us:
                mm_z(u)
        if k > 0:
            for u in us:
                mm_y(u - NH)
    for u in range(nu - NH, nu):
        mm_y(u)

    def relu(u):
        ve.wait_ge(sem["z%d" % u], 1)
        if u >= NH or not early:
            ve.wait_ge(sem["gb%d" % u], 1)
        if u >= RB:
            ve.wait_ge(sem["hs%d" % (u - RB)], 1)
        ve.tensor_tensor(hb[u % RB][:, :], ub[u % RB][:, 0:CW], T.zero[:, :], AluOpType.max).then_inc(sem["rl%d" % u], 1)

    def mult(u):
        ve.wait_ge(sem["rl%d" % u], 1)
        ve.wait_ge(sem["gb%d" % u], 1)
        ve.tensor_tensor(T.hs[:, u * CW:(u + 1) * CW], hb[u % RB][:, :], ub[u % RB][:, CW:2 * CW], AluOpType.mult).then_inc(sem["hs%d" % u], 1)

    ve.wait_ge(sem.zr, 1)
    if early:
        for u in range(NH):
            relu(u)
    ve.wait_ge(sem.gg, ng)
    ve.tensor_copy(T.gs[0:MW, :], T.gps[0:MW, :]).then_inc(sem.gcp, 1)
    if early:
        for u in range(NH):
            mult(u)
    for k in range(1 if early else 0, m):
        for c in range(NH):
            relu(k * NH + c)
        for c in range(NH):
            mult(k * NH + c)
    for c in range(NH):
        ve.wait_ge(sem["yc%d" % c], m)
        if helper is not None:
            ve.tensor_copy(T.ysb[:, cols(c)], ya[c][:, 0:CW]).then_inc(sem["cp%d" % c], 1)
            continue
        ve.wait_ge(sem["pa0%d" % c], nback)
        ve.tensor_tensor(ya[c][:, 0:CW], ya[c][:, 0:CW], T.part[:, c * CW:(c + 1) * CW], AluOpType.add).then_inc(sem["ad%d" % c], 1)
        ve.wait_ge(sem["ad%d" % c], 1)
        ve.wait_ge(sem["pa1%d" % c], nback)
        ve.tensor_tensor(T.ysb[:, cols(c)], ya[c][:, 0:CW], T.part[:, (NH + c) * CW:(NH + c + 1) * CW], AluOpType.add).then_inc(sem["cp%d" % c], 1)
        q = sy if c % 2 == 0 else sc
        q.wait_ge(sem["cp%d" % c], 1)
        q.dma_start(T.y[:, cols(c)], T.ysb[:, cols(c)]).then_inc(sem["st%d" % c], 16)
        q.wait_ge(sem["st%d" % c], 16)


def rank_program(g, core, T, topo):
    calls, cnt, work, xsend, back = _plan(T, topo)
    if core not in work:
        return
    r, mine, helper, early = work[core]
    rankcore = T.cores[r]
    nxa = len(xsend[rankcore][1])
    nback = len(back[xsend[rankcore][0][0]][1])
    _compute(g, core, T, r, mine, helper, early, cnt, nxa, nback)
    total = 0
    for s, trs in calls.get(core, []):
        if helper is None:
            g.wait_ge(T.sem.ldw, 32)
        else:
            g.wait_ge(T.sem["arr%d" % s], cnt[(core, s)])
        slot = T.wall[:, s * WB:(s + 1) * WB]
        total += _write(g, core, T, topo, trs, slot, slot, T.sem["arr%d" % s])
    if helper is None:
        g.wait_ge(T.sem.ldx, 16)
        g.wait_ge(T.sem.ldp, 32)
        total += _write(g, core, T, topo, [xsend[core]], T.xg[:, 0:XW], T.xg[:, 0:XW], T.sem.xa)
    else:
        home, en = back[core]
        for c in range(NH):
            g.wait_ge(T.sem["cp%d" % c], 1)
            total += _write(g, core, T, topo, [([home], en)], T.ysb[:, c * CW:(c + 1) * CW],
                            T.part[:, (helper * NH + c) * CW:(helper * NH + c + 1) * CW], T.sem["pa%d%d" % (helper, c)])
    g.wait_ge(T.sem.snd, total)
